import numpy as np
import ml_dtypes


def mxq(x, axis, fmt="e4m3"):
    dtype, down = {"e4m3": (ml_dtypes.float8_e4m3fn, 7), "e5m2": (ml_dtypes.float8_e5m2, 14)}[fmt]
    v = np.moveaxis(np.asarray(x, np.float32).astype(ml_dtypes.bfloat16).astype(np.float64), axis, -1)
    blocks = v.reshape(v.shape[:-1] + (-1, 32))
    amax = np.abs(blocks).max(-1, keepdims=True)
    byte = np.maximum(np.where(amax > 0, np.frexp(amax)[1] - 1 + 127, 0) - down, 1)
    scale = np.exp2(byte - 127.0)
    codes = (blocks / scale).astype(np.float32).astype(dtype).astype(np.float64)
    return np.moveaxis((codes * scale).reshape(v.shape), -1, axis)


WIDE = False


def mx_kscale(k):
    if not WIDE:
        return np.ones(k)
    levels = np.array([10, -10, 5, -5, 0])
    if k % 512:
        return np.exp2(np.random.permutation(np.resize(levels, k // 32))).repeat(32)
    a = np.empty((k // 512, 16))
    for p in range(k // 512):
        a[p, :8] = np.random.permutation(np.resize(levels, 8))
        for g in range(8):
            far = levels[np.abs(levels - a[p, g]) >= 10]
            a[p, g + 8] = far[np.random.randint(len(far))]
    return np.exp2(a.ravel()).repeat(32)


BF16 = ml_dtypes.bfloat16


def bf(x):
    return np.asarray(x, np.float32).astype(BF16)


def f64(x):
    return np.asarray(x).astype(np.float64)


N, L, F, H, P = 1024, 512, 1024, 512, 4
PH = P * H


def draw0():
    s, t = mx_kscale(L), mx_kscale(F)
    return {
        "x": bf(np.random.standard_normal((N, L)) * s),
        "fut": bf(np.random.standard_normal((N, P, H))),
        "w1": bf(np.random.standard_normal((L, F)) / np.sqrt(L) / s[:, None] * t),
        "w2": bf(np.random.standard_normal((F, PH)) * 1.4 / np.sqrt(F) / t[:, None]),
        "wsk": bf(np.random.standard_normal((L, PH)) / np.sqrt(L) / s[:, None]),
        "vp": bf(np.random.uniform(0.4, 0.8, P)),
        "wres": bf(np.random.standard_normal((L, H)) / np.sqrt(L) / s[:, None]),
    }


def residual_block(xq, w1, w2, wsk):
    h = np.maximum(xq @ mxq(f64(w1), 0, "e4m3"), 0.0)
    return (mxq(h, 1, "e4m3") @ mxq(f64(w2), 0, "e4m3")) + (xq @ mxq(f64(wsk), 0, "e4m3"))


def temporal_decoder(g, fut, vp):
    u = np.maximum(g + f64(fut), 0.0)
    return np.sum(f64(vp)[None, :, None] * u, axis=1)


def core(x, fut, w1, w2, wsk, vp, wres):
    xq = mxq(f64(x), 1, "e4m3")
    r = residual_block(xq, w1, w2, wsk)
    g = np.reshape(r, fut.shape)
    dec = temporal_decoder(g, fut, vp)
    return dec + (xq @ mxq(f64(wres), 0, "e4m3"))


def e4m3fn_bytes(y):
    return np.clip(np.asarray(y, np.float64), -448.0, 448.0).astype(np.float32).astype(ml_dtypes.float8_e4m3fn).view(np.uint8)


def e4m3fn_values(b):
    return np.asarray(b, np.uint8).view(ml_dtypes.float8_e4m3fn).astype(np.float64)


def setup_inputs():
    d = draw0()
    x0 = np.asarray(d['w2']).astype(np.float64)
    s = (np.max(np.abs(x0), axis=(1,), keepdims=True) / 448.0).astype(np.float32)
    out = {}
    for k, v in d.items():
        if k == 'w2':
            out['w2_bytes'] = e4m3fn_bytes(x0 / s.astype(np.float64))
            out['w2_scale'] = s
        else:
            out[k] = v
    return out


def reference(x, fut, w1, w2_bytes, w2_scale, wsk, vp, wres):
    return core(x, fut, w1, e4m3fn_values(w2_bytes) * w2_scale.astype(np.float64), wsk, vp, wres)

@@ -1,0 +1,295 @@
+from contextlib import ExitStack
+
+import concourse.mybir as mybir
+from concourse.masks import make_identity
+
+N, L, F, H, NP = 1024, 512, 1024, 512, 4
+FLOPS = 2 * N * (L * F + F * NP * H + L * NP * H + L * H)
+
+F32 = mybir.dt.float32
+BF16 = mybir.dt.bfloat16
+U32 = mybir.dt.uint32
+U8 = mybir.dt.uint8
+E4M3 = mybir.dt.float8_e4m3fn
+E4M3X4 = mybir.dt.float8_e4m3fn_x4
+ALU = mybir.AluOpType
+ACT = mybir.ActivationFunctionType
+
+P = 128
+T = 4
+HALF = 256
+PAIRS = N // (2 * P)
+IL_WSK = ["v","v","s","s","pe","s","s","s"]
+IL_W2 = [["v","v"],["s","v"],["s","s"],["s","s"],["s","s"],["s","s"],["s","s"],["s","s"]]
+IL_WRES = ["v","pe"]
+H_ENG = [[["s","s"],["s","s"]],[["s","s"],["s","s"]],[["s","v"],["s","s"]],[["s","s"],["s","v"]]]
+WIDEN = [["ssss","ssss"],["ssss","ssss"],["ssss","ssss"],["ssss","ssss"],["ssss","ssss"],["ssss","ssss"],["ssss","ssss"],["ssss","ssss"]]
+X_ENG = ["s","s","s","s"]
+LOADS = "w10 x0 x1 x2 x3 s v w11 m00 m10 k0 r f0 k1 f1 m11 k3 k2 m01 f2 f3"
+HEAD = "w0 x0 x1 h00 h10 w1 x2 x3 h20 b0 h11 h30 r b1 b2 h01 b3 h31"
+PHASE0 = ["","h21","",""]
+
+
+def tile_tideresidualencodertemporaldecoder_kernel(
+    tc, x, fut, w1, w2_bytes, w2_scale, wsk, vp, wres, out
+):
+    nc = tc.nc
+    with ExitStack() as ctx:
+        keep = ctx.enter_context(tc.tile_pool(name="keep", bufs=1))
+        work = ctx.enter_context(tc.tile_pool(name="work", bufs=2))
+        psum = ctx.enter_context(tc.psum_pool(name="psum", bufs=8))
+
+        x_sb = [keep.tile([P, 2, L], BF16, name=f"x_sb{i}") for i in range(PAIRS)]
+        w1_sb = [keep.tile([P, T, 512], BF16, name=f"w1_sb{g}") for g in range(2)]
+        wsk_sb = [keep.tile([P, T, 512], BF16, name=f"wsk_sb{p}") for p in range(NP)]
+        w2_sb = [[keep.tile([P, T, 1024], U8, name=f"w2_sb{g}_{pp}") for pp in range(2)] for g in range(2)]
+        wres_sb = keep.tile([P, T, 512], BF16, name="wres_sb")
+        fut_sb = [keep.tile([P, 8, 512], BF16, name=f"fut_sb{p}") for p in range(NP)]
+        scale_sb = keep.tile([P, 2, T], F32, name="scale_sb")
+        vp_sb = keep.tile([P, NP], BF16, name="vp_sb")
+
+        x_v = x.rearrange("(i c q) k -> i q c k", c=2, q=P)
+        w1_v = w1.rearrange("(p j) (g f) -> g p j f", j=T, g=2)
+        wsk_v = wsk.rearrange("(p j) (b n) -> b p j n", j=T, b=NP)
+        w2_v = w2_bytes.rearrange("(g p t) (b n) -> g b p t n", g=2, t=T, b=2)
+        fut_v = fut.rearrange("(c q) b n -> b q c n", q=P)
+
+        def load(dst, src):
+            nc.sync.dma_start(out=dst, in_=src)
+
+        pieces = {f"x{i}": (x_sb[i][:], x_v[i]) for i in range(PAIRS)}
+        pieces.update({f"w1{g}": (w1_sb[g][:], w1_v[g]) for g in range(2)})
+        pieces.update({f"k{p}": (wsk_sb[p][:], wsk_v[p]) for p in range(NP)})
+        pieces.update({f"f{p}": (fut_sb[p][:], fut_v[p]) for p in range(NP)})
+        pieces.update({f"m{g}{b}": (w2_sb[g][b][:], w2_v[g, b]) for g in range(2) for b in range(2)})
+        pieces["r"] = (wres_sb[:], wres.rearrange("(p j) n -> p j n", j=T))
+        pieces["s"] = (scale_sb[:], w2_scale.rearrange("(g p t) o -> p g (t o)", g=2, t=T))
+        pieces["v"] = (vp_sb[:], vp.partition_broadcast(P))
+        for k in LOADS.split():
+            load(*pieces[k])
+
+        dummy = keep.tile([P, 1], F32, name="dummy")
+        nc.gpsimd.memset(dummy[:], 0.0)
+        nc.scalar.activation(out=dummy[:], in_=dummy[:], func=ACT.Relu)
+        ident_f32 = keep.tile([P, P], F32, name="ident_f32")
+        make_identity(nc, ident_f32[:])
+        ident = keep.tile([P, P], BF16, name="ident")
+        make_identity(nc, ident[:])
+        v_col = keep.tile([P, NP], F32, name="v_col")
+        nc.gpsimd.tensor_copy(out=v_col[:], in_=vp_sb[:])
+        nv_col = keep.tile([P, NP], F32, name="nv_col")
+        nc.gpsimd.tensor_scalar(out=nv_col[:], in0=vp_sb[:], scalar1=-1.0, scalar2=0.0, op0=ALU.mult, op1=ALU.add)
+        diag = [keep.tile([P, P], BF16, name=f"diag{p}") for p in range(NP)]
+        for p in range(NP):
+            nc.gpsimd.tensor_scalar(
+                out=diag[p][:], in0=ident[:], scalar1=v_col[:, p : p + 1], scalar2=None, op0=ALU.mult
+            )
+
+        def codes(width, name):
+            return (
+                keep.tile([P, width], U32, name=name, align_bytes=64),
+                keep.tile([P, width], U8, name=name + "_s", align_bytes=64),
+            )
+
+        x_q = [codes(2 * P, f"x_q{i}") for i in range(PAIRS)]
+        h_q = [[codes(2 * P, f"h_q{i}_{g}") for g in range(2)] for i in range(PAIRS)]
+        w1_q = [codes(512, f"w1_q{g}") for g in range(2)]
+        wres_q = [codes(HALF, f"wres_q{j}") for j in range(2)]
+        wsk_q = [[codes(HALF, f"wsk_q{j}_{p}") for p in range(NP)] for j in range(2)]
+        w2_q = [[codes(2 * HALF, f"w2_q{j}_{p}") for p in range(NP)] for j in range(2)]
+
+        def quantize(dst, src):
+            nc.vector.quantize_mx(out=dst[0][:].bitcast(E4M3X4), scales=dst[1][:], in_=src)
+
+        def mm(out_ap, a, a0, b, b0, n, start, stop):
+            nc.tensor.matmul_mx(
+                out=out_ap,
+                lhsT=a[0][:, a0 : a0 + P].bitcast(E4M3X4),
+                lhsT_scale=a[1][:, a0 : a0 + P],
+                rhs=b[0][:, b0 : b0 + n].bitcast(E4M3X4),
+                rhs_scale=b[1][:, b0 : b0 + n],
+                start=start,
+                stop=stop,
+            )
+
+        def prep_x(i):
+            bank = psum.tile([P, 2, 2, P], F32, name="bank")
+            for c in range(2):
+                words = x_sb[i][:, c, :].bitcast(F32)
+                for u in range(2):
+                    nc.tensor.transpose(bank[:, c, u, :], words[:, u::2], ident_f32[:])
+            xg = work.tile([P, 2, P, T], BF16, name="xg", align_bytes=64)
+            (nc.scalar.copy if X_ENG[i] == "s" else nc.vector.tensor_copy)(
+                out=xg[:].rearrange("p c n t -> p (c n t)").bitcast(F32).rearrange("p (c n u) -> p c n u", c=2, u=2),
+                in_=bank[:].rearrange("p c u n -> p c n u"),
+            )
+            quantize(x_q[i], xg[:].rearrange("p c n t -> p (c n t)"))
+
+        def prep_w1(g):
+            wg = work.tile([P, T, P, T], BF16, name="w1g", align_bytes=64)
+            nc.vector.tensor_copy(out=wg[:], in_=w1_sb[g][:].rearrange("p j (m t) -> p t m j", t=T))
+            quantize(w1_q[g], wg[:].rearrange("p t m j -> p (t m j)"))
+
+        def hidden(i, g):
+            hg = work.tile([P, 2, P, T], BF16, name="hg", align_bytes=64)
+            for c in range(2):
+                bank = psum.tile([P, T, P], F32, name="bank")
+                for t in range(T):
+                    mm(bank[:, t, :], w1_q[g], t * P, x_q[i], c * P, P, True, True)
+                if H_ENG[i][g][c] == "s":
+                    nc.scalar.activation(out=hg[:, c], in_=bank[:].rearrange("p t n -> p n t"), func=ACT.Relu)
+                else:
+                    nc.vector.tensor_scalar(out=hg[:, c], in0=bank[:].rearrange("p t n -> p n t"), scalar1=0.0, scalar2=None, op0=ALU.max)
+            quantize(h_q[i][g], hg[:].rearrange("p c n t -> p (c n t)"))
+
+        def interleave(engine, dst, src):
+            if engine == "pe":
+                bank = psum.tile([P, HALF, T], BF16, name="bank")
+                for n0 in range(0, HALF, P):
+                    nc.tensor.matmul(
+                        bank[:, n0 : n0 + P, :].rearrange("p n j -> p (n j)"),
+                        lhsT=ident[:],
+                        rhs=src[:, :, n0 : n0 + P].rearrange("p j n -> p n j"),
+                        start=True,
+                        stop=True,
+                    )
+                nc.scalar.copy(out=dst, in_=bank[:])
+            else:
+                for n0 in range(0, HALF, 64) if engine == "g" else [None]:
+                    part = slice(n0, n0 + 64) if engine == "g" else slice(0, HALF)
+                    o = dst[:, part].rearrange("p (c i) j -> p c j i", i=4)
+                    a = src[:, :, part].rearrange("p j (c i) -> p c j i", i=4)
+                    if engine == "g":
+                        nc.gpsimd.tensor_scalar(out=o, in0=a, scalar1=1.0, scalar2=0.0, op0=ALU.mult, op1=ALU.add)
+                    elif engine == "v":
+                        nc.vector.tensor_copy(out=o, in_=a)
+                    else:
+                        nc.scalar.copy(out=o, in_=a)
+
+        def prep_wres(j):
+            wg = work.tile([P, HALF, T], BF16, name="wresg", align_bytes=64)
+            interleave(IL_WRES[j], wg[:], wres_sb[:, :, j * HALF : (j + 1) * HALF])
+            quantize(wres_q[j], wg[:].rearrange("p n t -> p (n t)"))
+
+        blocks = [(j, p) for j in range(2) for p in range(NP)]
+
+        def prep_block(b):
+            j, p = blocks[b]
+            wide = work.tile([P, 2, T, HALF], BF16, name="wide")
+            w2g = work.tile([P, 2, HALF, T], BF16, name="w2g", align_bytes=64)
+            col = (p % 2) * 512 + j * HALF
+
+            def widen(g):
+                for t in range(T):
+                    fp8 = w2_sb[g][p // 2][:, t, col : col + HALF].bitcast(E4M3)
+                    sc = scale_sb[:, g, t : t + 1]
+                    if WIDEN[b][g][t] == "s":
+                        nc.scalar.activation(out=wide[:, g, t, :], in_=fp8, func=ACT.Copy, scale=sc)
+                    else:
+                        nc.vector.tensor_scalar(out=wide[:, g, t, :], in0=fp8, scalar1=sc, scalar2=None, op0=ALU.mult)
+
+            wskg = work.tile([P, HALF, T], BF16, name="wskg", align_bytes=64)
+
+            def skip():
+                interleave(IL_WSK[b], wskg[:], wsk_sb[p][:, :, j * HALF : (j + 1) * HALF])
+
+            def w2_interleave(g):
+                interleave(IL_W2[b][g], w2g[:, g], wide[:, g])
+
+            def step0():
+                widen(0)
+                skip()
+
+            def step1():
+                widen(1)
+                quantize(wsk_q[j][p], wskg[:].rearrange("p n t -> p (n t)"))
+
+            def step2():
+                w2_interleave(0)
+                w2_interleave(1)
+
+            def step3():
+                quantize(w2_q[j][p], w2g[:].rearrange("p g n t -> p (g n t)"))
+
+            return [step0, step1, step2, step3]
+
+        acc = [[keep.tile([P, 2, HALF], F32, name=f"acc{j}_{i}") for i in range(PAIRS)] for j in range(2)]
+        flat = "p c n -> p (c n)"
+        sf_at = {0: 3, 1: 1}
+
+        def main_first(b, i):
+            j, p = blocks[b]
+            bank = psum.tile([P, 2, HALF], F32, name="bank")
+            for c in range(2):
+                mm(bank[:, c, :], x_q[i], c * P, wsk_q[j][p], 0, HALF, True, False)
+                mm(bank[:, c, :], h_q[i][0], c * P, w2_q[j][p], 0, HALF, False, False)
+                mm(bank[:, c, :], h_q[i][1], c * P, w2_q[j][p], HALF, HALF, False, True)
+            extra = None
+            if p == 0:
+                extra = psum.tile([P, 2, HALF], F32, name="bank")
+                for c in range(2):
+                    mm(extra[:, c, :], x_q[i], c * P, wres_q[j], 0, HALF, True, True)
+            elif p == sf_at[j]:
+                extra = psum.tile([P, 2, HALF], F32, name="bank")
+                for c in range(2):
+                    for q in range(NP):
+                        nc.tensor.matmul(
+                            extra[:, c, :],
+                            lhsT=diag[q][:],
+                            rhs=fut_sb[q][:, 2 * i + c, j * HALF : (j + 1) * HALF],
+                            start=(q == 0),
+                            stop=(q == NP - 1),
+                        )
+            m = work.tile([P, 2, HALF], F32, name="m", bufs=4)
+            nc.vector.scalar_tensor_tensor(
+                out=m[:],
+                in0=bank[:],
+                scalar=-1.0,
+                in1=fut_sb[p][:, 2 * i : 2 * i + 2, j * HALF : (j + 1) * HALF],
+                op0=ALU.mult,
+                op1=ALU.min,
+            )
+            return m, extra
+
+        def main_second(b, i, m, extra):
+            j, p = blocks[b]
+            a = acc[j][i]
+            if p == sf_at[j]:
+                nc.vector.tensor_tensor(out=a[:], in0=a[:], in1=extra[:], op=ALU.add)
+            nc.vector.scalar_tensor_tensor(
+                out=a[:],
+                in0=m[:],
+                scalar=nv_col[:, p : p + 1],
+                in1=extra[:] if p == 0 else a[:],
+                op0=ALU.mult,
+                op1=ALU.add,
+            )
+            if p == NP - 1:
+                nc.sync.dma_start(
+                    out=out.rearrange("(i c q) (j n) -> i j q c n", c=2, q=P, j=2)[i, j], in_=a[:]
+                )
+
+        first = prep_block(0)
+        todo = {f"x{i}": (lambda i=i: prep_x(i)) for i in range(PAIRS)}
+        todo.update({f"w{g}": (lambda g=g: prep_w1(g)) for g in range(2)})
+        todo.update({f"h{i}{g}": (lambda i=i, g=g: hidden(i, g)) for i in range(PAIRS) for g in range(2)})
+        todo.update({f"b{k}": first[k] for k in range(4)})
+        todo["r"] = lambda: prep_wres(0)
+        for k in HEAD.split():
+            todo[k]()
+        pending = None
+        for b in range(len(blocks)):
+            steps = prep_block(b + 1) if b + 1 < len(blocks) else None
+            for i in range(PAIRS):
+                done = main_first(b, i)
+                if b == 0:
+                    for k in PHASE0[i].split():
+                        todo[k]()
+                if steps:
+                    steps[i]()
+                if b == 2 and i == 0:
+                    prep_wres(1)
+                if pending:
+                    main_second(*pending)
+                pending = (b, i, done[0], done[1])
+        main_second(*pending)

@@ -19,15 +19,20 @@ P = 128
 T = 4
 HALF = 256
 PAIRS = N // (2 * P)
-IL_WSK = ["v","v","s","s","pe","s","s","s"]
-IL_W2 = [["v","v"],["s","v"],["s","s"],["s","s"],["s","s"],["s","s"],["s","s"],["s","s"]]
-IL_WRES = ["v","pe"]
-H_ENG = [[["s","s"],["s","s"]],[["s","s"],["s","s"]],[["s","v"],["s","s"]],[["s","s"],["s","v"]]]
-WIDEN = [["ssss","ssss"],["ssss","ssss"],["ssss","ssss"],["ssss","ssss"],["ssss","ssss"],["ssss","ssss"],["ssss","ssss"],["ssss","ssss"]]
+IL_WSK = ["v","s","s","s","s","s","s","s"]
+IL_W2 = [["s","v"],["v","s"],["s","s"],["s","s"],["s","s"],["s","s"],["s","s"],["s","s"]]
+IL_WRES = ["v","s"]
+H_ENG = [[["s","s"],["s","v"]],[["v","v"],["s","s"]],[["s","s"],["v","s"]],[["s","v"],["s","v"]]]
+WIDEN = [["vvss","vsss"],["ssss","ssss"],["ssss","ssss"],["ssss","vvvs"],["ssss","ssss"],["ssss","ssss"],["ssss","ssss"],["ssss","ssss"]]
 X_ENG = ["s","s","s","s"]
-LOADS = "w10 x0 x1 x2 x3 s v w11 m00 m10 k0 r f0 k1 f1 m11 k3 k2 m01 f2 f3"
-HEAD = "w0 x0 x1 h00 h10 w1 x2 x3 h20 b0 h11 h30 r b1 b2 h01 b3 h31"
-PHASE0 = ["","h21","",""]
+LOADS = "w10 x1 x0 x2 m00 x3 w11 f0 m10 r k0 k2 m11 k1 m01 f1 g0 g1"
+HEAD = "x1 V w0 x0 qx0 qx1 qw0 x2 qx2 w1 x3 h00 qx3 qw1 B0n0 qh00 h10 h20 h30 h01 B0i0 B0n1 qh20 r0 B1n0 r1 B0i1 qh10 qh30 B0k qr0 B0q B0qk h31 h11 qh01 h21 qh11 B1n1 B1i1 qh21 qr1 B1i0 qh31 B1k"
+FILL = {"B1qk":2,"B1q":3}
+OFFS = {"q":-2,"i1":-4,"n1":-8,"i0":-5,"qk":-4,"n0":-8,"k":-6}
+FORM = "bb"
+LAG = 1
+SF_AT = [3,1]
+MANUAL = True
 
 
 def tile_tideresidualencodertemporaldecoder_kernel(
@@ -41,30 +46,39 @@ def tile_tideresidualencodertemporaldecoder_kernel(
 
         x_sb = [keep.tile([P, 2, L], BF16, name=f"x_sb{i}") for i in range(PAIRS)]
         w1_sb = [keep.tile([P, T, 512], BF16, name=f"w1_sb{g}") for g in range(2)]
-        wsk_sb = [keep.tile([P, T, 512], BF16, name=f"wsk_sb{p}") for p in range(NP)]
+        wsk_lo = [keep.tile([P, T, 512], BF16, name=f"wsk_sb{p}") for p in range(2)]
+        wsk_hi = keep.tile([P, T, 1024], BF16, name="wsk_hi")
+        wsk_sb = [wsk_lo[0][:], wsk_lo[1][:], wsk_hi[:, :, 0:512], wsk_hi[:, :, 512:1024]]
         w2_sb = [[keep.tile([P, T, 1024], U8, name=f"w2_sb{g}_{pp}") for pp in range(2)] for g in range(2)]
         wres_sb = keep.tile([P, T, 512], BF16, name="wres_sb")
-        fut_sb = [keep.tile([P, 8, 512], BF16, name=f"fut_sb{p}") for p in range(NP)]
+        fut_lo = [keep.tile([P, 8, 512], BF16, name=f"fut_sb{p}") for p in range(2)]
+        fut_hi = keep.tile([P, 8, 2, 512], BF16, name="fut_hi")
+        fut_sb = [fut_lo[0][:], fut_lo[1][:], fut_hi[:, :, 0, :], fut_hi[:, :, 1, :]]
         scale_sb = keep.tile([P, 2, T], F32, name="scale_sb")
         vp_sb = keep.tile([P, NP], BF16, name="vp_sb")
+        nc.vector.memset(vp_sb[:], 0.0)
 
-        x_v = x.rearrange("(i c q) k -> i q c k", c=2, q=P)
+        x_v = x.rearrange("(q i c) k -> i q c k", c=2, i=PAIRS)
         w1_v = w1.rearrange("(p j) (g f) -> g p j f", j=T, g=2)
         wsk_v = wsk.rearrange("(p j) (b n) -> b p j n", j=T, b=NP)
         w2_v = w2_bytes.rearrange("(g p t) (b n) -> g b p t n", g=2, t=T, b=2)
-        fut_v = fut.rearrange("(c q) b n -> b q c n", q=P)
+        fut_v = fut.rearrange("(q c) b n -> b q c n", q=P)
+        fut_hv = fut.rearrange("(q c) (h b) n -> h q c b n", q=P, h=2)
+        wsk_hv = wsk.rearrange("(p j) (h n) -> h p j n", j=T, h=2)
 
         def load(dst, src):
             nc.sync.dma_start(out=dst, in_=src)
 
         pieces = {f"x{i}": (x_sb[i][:], x_v[i]) for i in range(PAIRS)}
         pieces.update({f"w1{g}": (w1_sb[g][:], w1_v[g]) for g in range(2)})
-        pieces.update({f"k{p}": (wsk_sb[p][:], wsk_v[p]) for p in range(NP)})
-        pieces.update({f"f{p}": (fut_sb[p][:], fut_v[p]) for p in range(NP)})
+        pieces.update({f"k{p}": (wsk_lo[p][:], wsk_v[p]) for p in range(2)})
+        pieces.update({f"f{p}": (fut_lo[p][:], fut_v[p]) for p in range(2)})
         pieces.update({f"m{g}{b}": (w2_sb[g][b][:], w2_v[g, b]) for g in range(2) for b in range(2)})
+        pieces["k2"] = (wsk_hi[:], wsk_hv[1])
+        pieces.update({f"g{h}": (fut_hi[:, 4 * h : 4 * h + 4], fut_hv[1][:, 4 * h : 4 * h + 4]) for h in range(2)})
         pieces["r"] = (wres_sb[:], wres.rearrange("(p j) n -> p j n", j=T))
-        pieces["s"] = (scale_sb[:], w2_scale.rearrange("(g p t) o -> p g (t o)", g=2, t=T))
-        pieces["v"] = (vp_sb[:], vp.partition_broadcast(P))
+        nc.scalar.dma_start(out=scale_sb[:], in_=w2_scale.rearrange("(g p t) o -> p g (t o)", g=2, t=T))
+        nc.scalar.dma_start(out=vp_sb[0:1, :], in_=vp.rearrange("(o n) -> o n", o=1))
         for k in LOADS.split():
             load(*pieces[k])
 
@@ -75,15 +89,21 @@ def tile_tideresidualencodertemporaldecoder_kernel(
         make_identity(nc, ident_f32[:])
         ident = keep.tile([P, P], BF16, name="ident")
         make_identity(nc, ident[:])
+        ones = keep.tile([P, P], BF16, name="ones")
+        nc.gpsimd.memset(ones[:], 1.0)
         v_col = keep.tile([P, NP], F32, name="v_col")
-        nc.gpsimd.tensor_copy(out=v_col[:], in_=vp_sb[:])
         nv_col = keep.tile([P, NP], F32, name="nv_col")
-        nc.gpsimd.tensor_scalar(out=nv_col[:], in0=vp_sb[:], scalar1=-1.0, scalar2=0.0, op0=ALU.mult, op1=ALU.add)
         diag = [keep.tile([P, P], BF16, name=f"diag{p}") for p in range(NP)]
-        for p in range(NP):
-            nc.gpsimd.tensor_scalar(
-                out=diag[p][:], in0=ident[:], scalar1=v_col[:, p : p + 1], scalar2=None, op0=ALU.mult
-            )
+
+        def spread_v():
+            bank = psum.tile([P, NP], F32, name="bank")
+            nc.tensor.matmul(bank[:], lhsT=ones[:], rhs=vp_sb[:], start=True, stop=True)
+            nc.scalar.copy(out=v_col[:], in_=bank[:])
+            nc.scalar.activation(out=nv_col[:], in_=v_col[:], func=ACT.Copy, scale=-1.0)
+            for p in range(NP):
+                nc.gpsimd.tensor_scalar(
+                    out=diag[p][:], in0=ident[:], scalar1=v_col[:, p : p + 1], scalar2=0.0, op0=ALU.mult, op1=ALU.add
+                )
 
         def codes(width, name):
             return (
@@ -112,26 +132,28 @@ def tile_tideresidualencodertemporaldecoder_kernel(
                 stop=stop,
             )
 
+        later = {}
+
         def prep_x(i):
             bank = psum.tile([P, 2, 2, P], F32, name="bank")
             for c in range(2):
                 words = x_sb[i][:, c, :].bitcast(F32)
                 for u in range(2):
                     nc.tensor.transpose(bank[:, c, u, :], words[:, u::2], ident_f32[:])
-            xg = work.tile([P, 2, P, T], BF16, name="xg", align_bytes=64)
+            xg = work.tile([P, 2, P, T], BF16, name="xg", align_bytes=64, bufs=3)
             (nc.scalar.copy if X_ENG[i] == "s" else nc.vector.tensor_copy)(
                 out=xg[:].rearrange("p c n t -> p (c n t)").bitcast(F32).rearrange("p (c n u) -> p c n u", c=2, u=2),
                 in_=bank[:].rearrange("p c u n -> p c n u"),
             )
-            quantize(x_q[i], xg[:].rearrange("p c n t -> p (c n t)"))
+            later[f"x{i}"] = lambda: quantize(x_q[i], xg[:].rearrange("p c n t -> p (c n t)"))
 
         def prep_w1(g):
             wg = work.tile([P, T, P, T], BF16, name="w1g", align_bytes=64)
             nc.vector.tensor_copy(out=wg[:], in_=w1_sb[g][:].rearrange("p j (m t) -> p t m j", t=T))
-            quantize(w1_q[g], wg[:].rearrange("p t m j -> p (t m j)"))
+            later[f"w{g}"] = lambda: quantize(w1_q[g], wg[:].rearrange("p t m j -> p (t m j)"))
 
         def hidden(i, g):
-            hg = work.tile([P, 2, P, T], BF16, name="hg", align_bytes=64)
+            hg = work.tile([P, 2, P, T], BF16, name="hg", align_bytes=64, bufs=4)
             for c in range(2):
                 bank = psum.tile([P, T, P], F32, name="bank")
                 for t in range(T):
@@ -140,7 +162,7 @@ def tile_tideresidualencodertemporaldecoder_kernel(
                     nc.scalar.activation(out=hg[:, c], in_=bank[:].rearrange("p t n -> p n t"), func=ACT.Relu)
                 else:
                     nc.vector.tensor_scalar(out=hg[:, c], in0=bank[:].rearrange("p t n -> p n t"), scalar1=0.0, scalar2=None, op0=ALU.max)
-            quantize(h_q[i][g], hg[:].rearrange("p c n t -> p (c n t)"))
+            later[f"h{i}{g}"] = lambda: quantize(h_q[i][g], hg[:].rearrange("p c n t -> p (c n t)"))
 
         def interleave(engine, dst, src):
             if engine == "pe":
@@ -169,14 +191,15 @@ def tile_tideresidualencodertemporaldecoder_kernel(
         def prep_wres(j):
             wg = work.tile([P, HALF, T], BF16, name="wresg", align_bytes=64)
             interleave(IL_WRES[j], wg[:], wres_sb[:, :, j * HALF : (j + 1) * HALF])
-            quantize(wres_q[j], wg[:].rearrange("p n t -> p (n t)"))
+            later[f"r{j}"] = lambda: quantize(wres_q[j], wg[:].rearrange("p n t -> p (n t)"))
 
         blocks = [(j, p) for j in range(2) for p in range(NP)]
 
         def prep_block(b):
             j, p = blocks[b]
-            wide = work.tile([P, 2, T, HALF], BF16, name="wide")
-            w2g = work.tile([P, 2, HALF, T], BF16, name="w2g", align_bytes=64)
+            wide = work.tile([P, 2, T, HALF], BF16, name="wide", bufs=3)
+            w2g = work.tile([P, 2, HALF, T], BF16, name="w2g", align_bytes=64, bufs=3)
+            wskg = work.tile([P, HALF, T], BF16, name="wskg", align_bytes=64, bufs=3)
             col = (p % 2) * 512 + j * HALF
 
             def widen(g):
@@ -188,36 +211,20 @@ def tile_tideresidualencodertemporaldecoder_kernel(
                     else:
                         nc.vector.tensor_scalar(out=wide[:, g, t, :], in0=fp8, scalar1=sc, scalar2=None, op0=ALU.mult)
 
-            wskg = work.tile([P, HALF, T], BF16, name="wskg", align_bytes=64)
-
-            def skip():
-                interleave(IL_WSK[b], wskg[:], wsk_sb[p][:, :, j * HALF : (j + 1) * HALF])
-
-            def w2_interleave(g):
-                interleave(IL_W2[b][g], w2g[:, g], wide[:, g])
-
-            def step0():
-                widen(0)
-                skip()
-
-            def step1():
-                widen(1)
-                quantize(wsk_q[j][p], wskg[:].rearrange("p n t -> p (n t)"))
-
-            def step2():
-                w2_interleave(0)
-                w2_interleave(1)
-
-            def step3():
-                quantize(w2_q[j][p], w2g[:].rearrange("p g n t -> p (g n t)"))
-
-            return [step0, step1, step2, step3]
+            return {
+                "n0": lambda: widen(0),
+                "n1": lambda: widen(1),
+                "k": lambda: interleave(IL_WSK[b], wskg[:], wsk_sb[p][:, :, j * HALF : (j + 1) * HALF]),
+                "i0": lambda: interleave(IL_W2[b][0], w2g[:, 0], wide[:, 0]),
+                "i1": lambda: interleave(IL_W2[b][1], w2g[:, 1], wide[:, 1]),
+                "qk": lambda: quantize(wsk_q[j][p], wskg[:].rearrange("p n t -> p (n t)")),
+                "q": lambda: quantize(w2_q[j][p], w2g[:].rearrange("p g n t -> p (g n t)")),
+            }
 
         acc = [[keep.tile([P, 2, HALF], F32, name=f"acc{j}_{i}") for i in range(PAIRS)] for j in range(2)]
         flat = "p c n -> p (c n)"
-        sf_at = {0: 3, 1: 1}
 
-        def main_first(b, i):
+        def multiply(b, i):
             j, p = blocks[b]
             bank = psum.tile([P, 2, HALF], F32, name="bank")
             for c in range(2):
@@ -229,7 +236,7 @@ def tile_tideresidualencodertemporaldecoder_kernel(
                 extra = psum.tile([P, 2, HALF], F32, name="bank")
                 for c in range(2):
                     mm(extra[:, c, :], x_q[i], c * P, wres_q[j], 0, HALF, True, True)
-            elif p == sf_at[j]:
+            elif FORM[j] == "b" and p == SF_AT[j]:
                 extra = psum.tile([P, 2, HALF], F32, name="bank")
                 for c in range(2):
                     for q in range(NP):
@@ -240,56 +247,87 @@ def tile_tideresidualencodertemporaldecoder_kernel(
                             start=(q == 0),
                             stop=(q == NP - 1),
                         )
-            m = work.tile([P, 2, HALF], F32, name="m", bufs=4)
-            nc.vector.scalar_tensor_tensor(
-                out=m[:],
-                in0=bank[:],
-                scalar=-1.0,
-                in1=fut_sb[p][:, 2 * i : 2 * i + 2, j * HALF : (j + 1) * HALF],
-                op0=ALU.mult,
-                op1=ALU.min,
-            )
-            return m, extra
+            return bank, extra
 
-        def main_second(b, i, m, extra):
+        def first_pass(b, i, bank):
+            j, p = blocks[b]
+            m = work.tile([P, 2, HALF], F32, name="m", bufs=6)
+            f = fut_sb[p][:, 2 * i : 2 * i + 2, j * HALF : (j + 1) * HALF]
+            if FORM[j] == "b":
+                nc.vector.scalar_tensor_tensor(out=m[:], in0=bank[:], scalar=-1.0, in1=f, op0=ALU.mult, op1=ALU.min)
+            else:
+                z = work.tile([P, 2, HALF], F32, name="z", bufs=4)
+                nc.vector.tensor_tensor(out=z[:], in0=bank[:], in1=f, op=ALU.add)
+                nc.scalar.activation(out=m[:], in_=z[:], func=ACT.Relu)
+            return m
+
+        def add_sf(b, i, extra):
+            j, p = blocks[b]
+            if FORM[j] == "b" and p == SF_AT[j]:
+                a = acc[j][i]
+                nc.vector.tensor_tensor(out=a[:], in0=a[:], in1=extra[:], op=ALU.add)
+
+        def second_pass(b, i, m, extra):
             j, p = blocks[b]
             a = acc[j][i]
-            if p == sf_at[j]:
-                nc.vector.tensor_tensor(out=a[:], in0=a[:], in1=extra[:], op=ALU.add)
             nc.vector.scalar_tensor_tensor(
                 out=a[:],
                 in0=m[:],
-                scalar=nv_col[:, p : p + 1],
+                scalar=(nv_col if FORM[j] == "b" else v_col)[:, p : p + 1],
                 in1=extra[:] if p == 0 else a[:],
                 op0=ALU.mult,
                 op1=ALU.add,
             )
             if p == NP - 1:
                 nc.sync.dma_start(
-                    out=out.rearrange("(i c q) (j n) -> i j q c n", c=2, q=P, j=2)[i, j], in_=a[:]
+                    out=out.rearrange("(q i c) (j n) -> i j q c n", c=2, i=PAIRS, j=2)[i, j], in_=a[:]
                 )
 
-        first = prep_block(0)
-        todo = {f"x{i}": (lambda i=i: prep_x(i)) for i in range(PAIRS)}
-        todo.update({f"w{g}": (lambda g=g: prep_w1(g)) for g in range(2)})
-        todo.update({f"h{i}{g}": (lambda i=i, g=g: hidden(i, g)) for i in range(PAIRS) for g in range(2)})
-        todo.update({f"b{k}": first[k] for k in range(4)})
-        todo["r"] = lambda: prep_wres(0)
+        if MANUAL:
+            ctx.enter_context(tc.manual_schedule())
+        todo = {"V": spread_v}
+        for i in range(PAIRS):
+            todo[f"x{i}"] = lambda i=i: prep_x(i)
+            for g in range(2):
+                todo[f"h{i}{g}"] = lambda i=i, g=g: hidden(i, g)
+        for g in range(2):
+            todo[f"w{g}"] = lambda g=g: prep_w1(g)
+            todo[f"r{g}"] = lambda g=g: prep_wres(g)
+        preps = {}
+
+        def emit(k):
+            if k[0] == "B":
+                b = int(k[1])
+                if b not in preps:
+                    preps[b] = prep_block(b)
+                preps[b][k[2:]]()
+            elif k[0] == "q":
+                later[k[1:]]()
+            else:
+                todo[k]()
+
         for k in HEAD.split():
-            todo[k]()
-        pending = None
-        for b in range(len(blocks)):
-            steps = prep_block(b + 1) if b + 1 < len(blocks) else None
-            for i in range(PAIRS):
-                done = main_first(b, i)
-                if b == 0:
-                    for k in PHASE0[i].split():
-                        todo[k]()
-                if steps:
-                    steps[i]()
-                if b == 2 and i == 0:
-                    prep_wres(1)
-                if pending:
-                    main_second(*pending)
-                pending = (b, i, done[0], done[1])
-        main_second(*pending)
+            emit(k)
+        fill = {}
+        for k, at in FILL.items():
+            fill.setdefault(at, []).append(k)
+        for b in range(2, len(blocks)):
+            for k, at in OFFS.items():
+                fill.setdefault(4 * b + at, []).append(f"B{b}{k}")
+        pending = []
+        for st in range(4 * len(blocks)):
+            b, i = divmod(st, PAIRS)
+            bank, extra = multiply(b, i)
+            for k in fill.get(st, []):
+                if k[2:] not in ("q", "qk") and k[0] != "q":
+                    emit(k)
+            m = first_pass(b, i, bank)
+            for k in fill.get(st, []):
+                if k[2:] in ("q", "qk") or k[0] == "q":
+                    emit(k)
+            if len(pending) >= LAG:
+                second_pass(*pending.pop(0))
+            add_sf(b, i, extra)
+            pending.append((b, i, m, extra))
+        for q in pending:
+            second_pass(*q)

@@ -20,18 +20,14 @@ T = 4
 HALF = 256
 PAIRS = N // (2 * P)
 IL_WSK = ["v","s","s","s","s","s","s","s"]
-IL_W2 = [["s","v"],["v","s"],["s","s"],["s","s"],["s","s"],["s","s"],["s","s"],["s","s"]]
-IL_WRES = ["v","s"]
-H_ENG = [[["s","s"],["s","v"]],[["v","v"],["s","s"]],[["s","s"],["v","s"]],[["s","v"],["s","v"]]]
-WIDEN = [["vvss","vsss"],["ssss","ssss"],["ssss","ssss"],["ssss","vvvs"],["ssss","ssss"],["ssss","ssss"],["ssss","ssss"],["ssss","ssss"]]
-X_ENG = ["s","s","s","s"]
-LOADS = "w10 x1 x0 x2 m00 x3 w11 f0 m10 r k0 k2 m11 k1 m01 f1 g0 g1"
-HEAD = "x1 V w0 x0 qx0 qx1 qw0 x2 qx2 w1 x3 h00 qx3 qw1 B0n0 qh00 h10 h20 h30 h01 B0i0 B0n1 qh20 r0 B1n0 r1 B0i1 qh10 qh30 B0k qr0 B0q B0qk h31 h11 qh01 h21 qh11 B1n1 B1i1 qh21 qr1 B1i0 qh31 B1k"
-FILL = {"B1qk":2,"B1q":3}
-OFFS = {"q":-2,"i1":-4,"n1":-8,"i0":-5,"qk":-4,"n0":-8,"k":-6}
-FORM = "bb"
-LAG = 1
-SF_AT = [3,1]
+IL_W2 = [["s","s"],["s","s"],["s","s"],["s","v"],["v","v"],["s","s"],["s","s"],["s","s"]]
+IL_WRES = ["s","v"]
+H_ENG = [[["s","s"],["s","s"]],[["s","s"],["s","s"]],[["s","v"],["s","s"]],[["v","s"],["s","s"]]]
+X_ENG = ["s","v","s","s"]
+WIDEN = [["ssss","ssss"],["ssss","vvvv"],["ssss","ssss"],["ssss","ssss"],["vvvv","vvvv"],["ssss","ssss"],["ssss","ssss"],["ssss","ssss"]]
+PE_P2 = [[[],[1],[1],[]],[[2],[],[1],[2]]]
+LOADS = "m00 w11 m10 x3 x1 w10 r x2 k0 f0 x0 g1 m11 k1 m02 m01 f1 k2 m12 g0"
+ORDER = "B4n0 B0n0 B4i0 B0i0 w1 B0n1 B4n1 X3 qw1 X1 x3 V B4i1 B0i1 qx3 B4q H310 H311 x1 h310 B0q h311 qx1 r0 X2 qh31 w0 H110 H111 x2 B4k qr0 qw0 W1 W3 qx2 H100 r1 h110 H200 H201 h200 B4qk H101 h201 H300 h111 B0k h100 H301 h300 h101 X0 B0qk h301 H210 qh10 qh11 x0 H211 qh30 M1 h210 qr1 qx0 h211 qh20 H000 P1 H001 h000 H010 B1n1 H011 h001 M3 qh21 h010 S1 M2 h011 qh00 P3 B1i1 W0 qh01 M17 P2 S3 B1k M0 P17 W2 P0 M16 B1n0 B1qk S0 M18 B3n0 S2 W16 P16 W17 M19 B1i0 P18 S16 P19 B3i0 F03 S17 B1q W18 B3k S18 M4 A03 B2n1 M5 B3qk P4 M6 P5 B3n1 S4 M7 P6 B5n0 F00 B3i1 P7 B5k F11 B3q S7 B6n0 M12 B5qk A00 M13 B5n1 P12 M14 A11 B5i0 P13 M15 P14 W19 S12 B5i1 F02 S13 S14 B6k B5q S19 M20 B6n1 B6qk P15 M21 B6i0 P20 M22 S15 P21 B6i1 M23 P22 F01 S20 B7k B6q P23 B2k B7qk S21 M24 S23 B2n0 M25 P24 B2qk M26 B2i1 P25 A02 M27 B2i0 P26 F10 P27 S25 B7n0 B2q S26 B7n1 M8 A10 A01 M9 B7i0 P8 M10 P9 B7i1 S8 M11 P10 F12 B7q P11 S9 S10 M28 S11 M29 A12 P28 M30 P29 M31 S28 P30 F13 P31 S29 S30 S31 A13"
 MANUAL = True
 
 
@@ -42,16 +38,18 @@ def tile_tideresidualencodertemporaldecoder_kernel(
     with ExitStack() as ctx:
         keep = ctx.enter_context(tc.tile_pool(name="keep", bufs=1))
         work = ctx.enter_context(tc.tile_pool(name="work", bufs=2))
-        psum = ctx.enter_context(tc.psum_pool(name="psum", bufs=8))
+        psum = ctx.enter_context(tc.psum_pool(name="psum", bufs=6))
 
         x_sb = [keep.tile([P, 2, L], BF16, name=f"x_sb{i}") for i in range(PAIRS)]
         w1_sb = [keep.tile([P, T, 512], BF16, name=f"w1_sb{g}") for g in range(2)]
         wsk_lo = [keep.tile([P, T, 512], BF16, name=f"wsk_sb{p}") for p in range(2)]
         wsk_hi = keep.tile([P, T, 1024], BF16, name="wsk_hi")
         wsk_sb = [wsk_lo[0][:], wsk_lo[1][:], wsk_hi[:, :, 0:512], wsk_hi[:, :, 512:1024]]
-        w2_sb = [[keep.tile([P, T, 1024], U8, name=f"w2_sb{g}_{pp}") for pp in range(2)] for g in range(2)]
+        w2_lo = [[keep.tile([P, T, 512], U8, name=f"w2_lo{g}_{p}") for p in range(2)] for g in range(2)]
+        w2_hi = [keep.tile([P, T, 1024], U8, name=f"w2_hi{g}") for g in range(2)]
+        w2_sb = [[w2_lo[g][0][:], w2_lo[g][1][:], w2_hi[g][:, :, 0:512], w2_hi[g][:, :, 512:1024]] for g in range(2)]
         wres_sb = keep.tile([P, T, 512], BF16, name="wres_sb")
-        fut_lo = [keep.tile([P, 8, 512], BF16, name=f"fut_sb{p}") for p in range(2)]
+        fut_lo = [keep.tile([P, 8, 512], BF16, name=f"fut_lo{p}") for p in range(2)]
         fut_hi = keep.tile([P, 8, 2, 512], BF16, name="fut_hi")
         fut_sb = [fut_lo[0][:], fut_lo[1][:], fut_hi[:, :, 0, :], fut_hi[:, :, 1, :]]
         scale_sb = keep.tile([P, 2, T], F32, name="scale_sb")
@@ -61,7 +59,8 @@ def tile_tideresidualencodertemporaldecoder_kernel(
         x_v = x.rearrange("(q i c) k -> i q c k", c=2, i=PAIRS)
         w1_v = w1.rearrange("(p j) (g f) -> g p j f", j=T, g=2)
         wsk_v = wsk.rearrange("(p j) (b n) -> b p j n", j=T, b=NP)
-        w2_v = w2_bytes.rearrange("(g p t) (b n) -> g b p t n", g=2, t=T, b=2)
+        w2_v = w2_bytes.rearrange("(g p t) (b n) -> g b p t n", g=2, t=T, b=4)
+        w2_hv = w2_bytes.rearrange("(g p t) (b n) -> g b p t n", g=2, t=T, b=2)
         fut_v = fut.rearrange("(q c) b n -> b q c n", q=P)
         fut_hv = fut.rearrange("(q c) (h b) n -> h q c b n", q=P, h=2)
         wsk_hv = wsk.rearrange("(p j) (h n) -> h p j n", j=T, h=2)
@@ -73,9 +72,10 @@ def tile_tideresidualencodertemporaldecoder_kernel(
         pieces.update({f"w1{g}": (w1_sb[g][:], w1_v[g]) for g in range(2)})
         pieces.update({f"k{p}": (wsk_lo[p][:], wsk_v[p]) for p in range(2)})
         pieces.update({f"f{p}": (fut_lo[p][:], fut_v[p]) for p in range(2)})
-        pieces.update({f"m{g}{b}": (w2_sb[g][b][:], w2_v[g, b]) for g in range(2) for b in range(2)})
-        pieces["k2"] = (wsk_hi[:], wsk_hv[1])
         pieces.update({f"g{h}": (fut_hi[:, 4 * h : 4 * h + 4], fut_hv[1][:, 4 * h : 4 * h + 4]) for h in range(2)})
+        pieces.update({f"m{g}{b}": (w2_lo[g][b][:], w2_v[g, b]) for g in range(2) for b in range(2)})
+        pieces.update({f"m{g}2": (w2_hi[g][:], w2_hv[g, 1]) for g in range(2)})
+        pieces["k2"] = (wsk_hi[:], wsk_hv[1])
         pieces["r"] = (wres_sb[:], wres.rearrange("(p j) n -> p j n", j=T))
         nc.scalar.dma_start(out=scale_sb[:], in_=w2_scale.rearrange("(g p t) o -> p g (t o)", g=2, t=T))
         nc.scalar.dma_start(out=vp_sb[0:1, :], in_=vp.rearrange("(o n) -> o n", o=1))
@@ -93,13 +93,19 @@ def tile_tideresidualencodertemporaldecoder_kernel(
         nc.gpsimd.memset(ones[:], 1.0)
         v_col = keep.tile([P, NP], F32, name="v_col")
         nv_col = keep.tile([P, NP], F32, name="nv_col")
+        kept_m = {}
+        ndiag = {p: keep.tile([P, P], F32, name=f"ndiag{p}") for p in sorted({q for r in PE_P2 for t in r for q in t})}
         diag = [keep.tile([P, P], BF16, name=f"diag{p}") for p in range(NP)]
 
         def spread_v():
-            bank = psum.tile([P, NP], F32, name="bank")
+            bank = psum.tile([P, NP], F32, name="extra", bufs=2)
             nc.tensor.matmul(bank[:], lhsT=ones[:], rhs=vp_sb[:], start=True, stop=True)
             nc.scalar.copy(out=v_col[:], in_=bank[:])
             nc.scalar.activation(out=nv_col[:], in_=v_col[:], func=ACT.Copy, scale=-1.0)
+            for p in ndiag:
+                nc.gpsimd.tensor_scalar(
+                    out=ndiag[p][:], in0=ident_f32[:], scalar1=nv_col[:, p : p + 1], scalar2=0.0, op0=ALU.mult, op1=ALU.add
+                )
             for p in range(NP):
                 nc.gpsimd.tensor_scalar(
                     out=diag[p][:], in0=ident[:], scalar1=v_col[:, p : p + 1], scalar2=0.0, op0=ALU.mult, op1=ALU.add
@@ -134,13 +140,18 @@ def tile_tideresidualencodertemporaldecoder_kernel(
 
         later = {}
 
-        def prep_x(i):
-            bank = psum.tile([P, 2, 2, P], F32, name="bank")
+        x_banks, h_banks = {}, {}
+
+        def turn_x(i):
+            bank = x_banks[i] = psum.tile([P, 2, 2, P], F32, name="bank")
             for c in range(2):
                 words = x_sb[i][:, c, :].bitcast(F32)
                 for u in range(2):
                     nc.tensor.transpose(bank[:, c, u, :], words[:, u::2], ident_f32[:])
-            xg = work.tile([P, 2, P, T], BF16, name="xg", align_bytes=64, bufs=3)
+
+        def copy_x(i):
+            bank = x_banks[i]
+            xg = work.tile([P, 2, P, T], BF16, name="xg", align_bytes=64, bufs=4)
             (nc.scalar.copy if X_ENG[i] == "s" else nc.vector.tensor_copy)(
                 out=xg[:].rearrange("p c n t -> p (c n t)").bitcast(F32).rearrange("p (c n u) -> p c n u", c=2, u=2),
                 in_=bank[:].rearrange("p c u n -> p c n u"),
@@ -152,20 +163,30 @@ def tile_tideresidualencodertemporaldecoder_kernel(
             nc.vector.tensor_copy(out=wg[:], in_=w1_sb[g][:].rearrange("p j (m t) -> p t m j", t=T))
             later[f"w{g}"] = lambda: quantize(w1_q[g], wg[:].rearrange("p t m j -> p (t m j)"))
 
-        def hidden(i, g):
-            hg = work.tile([P, 2, P, T], BF16, name="hg", align_bytes=64, bufs=4)
-            for c in range(2):
-                bank = psum.tile([P, T, P], F32, name="bank")
+        def hidden(i, g, c):
+            if True:
+                bank = h_banks[i, g, c] = psum.tile([P, T, P], F32, name="bank")
                 for t in range(T):
                     mm(bank[:, t, :], w1_q[g], t * P, x_q[i], c * P, P, True, True)
+
+        h_tiles = {}
+
+        def copy_h(i, g, c):
+            if (i, g) not in h_tiles:
+                h_tiles[i, g] = work.tile([P, 2, P, T], BF16, name="hg", align_bytes=64, bufs=6)
+                later[f"h{i}{g}"] = lambda: quantize(h_q[i][g], h_tiles[i, g][:].rearrange("p c n t -> p (c n t)"))
+            hg = h_tiles[i, g]
+            if True:
+                bank = h_banks[i, g, c]
                 if H_ENG[i][g][c] == "s":
                     nc.scalar.activation(out=hg[:, c], in_=bank[:].rearrange("p t n -> p n t"), func=ACT.Relu)
                 else:
                     nc.vector.tensor_scalar(out=hg[:, c], in0=bank[:].rearrange("p t n -> p n t"), scalar1=0.0, scalar2=None, op0=ALU.max)
-            later[f"h{i}{g}"] = lambda: quantize(h_q[i][g], hg[:].rearrange("p c n t -> p (c n t)"))
 
-        def interleave(engine, dst, src):
-            if engine == "pe":
+        spread_banks = {}
+
+        def interleave(engine, dst, src, key=None):
+            if engine == "T":
                 bank = psum.tile([P, HALF, T], BF16, name="bank")
                 for n0 in range(0, HALF, P):
                     nc.tensor.matmul(
@@ -175,10 +196,13 @@ def tile_tideresidualencodertemporaldecoder_kernel(
                         start=True,
                         stop=True,
                     )
-                nc.scalar.copy(out=dst, in_=bank[:])
+                return bank
+            elif engine == "pe":
+                nc.scalar.copy(out=dst, in_=spread_banks[key][:])
             else:
-                for n0 in range(0, HALF, 64) if engine == "g" else [None]:
-                    part = slice(n0, n0 + 64) if engine == "g" else slice(0, HALF)
+                cuts = [0, 88, 172, HALF] if engine == "g" else [0, HALF]
+                for n0, n1 in zip(cuts, cuts[1:]):
+                    part = slice(n0, n1)
                     o = dst[:, part].rearrange("p (c i) j -> p c j i", i=4)
                     a = src[:, :, part].rearrange("p j (c i) -> p c j i", i=4)
                     if engine == "g":
@@ -189,36 +213,43 @@ def tile_tideresidualencodertemporaldecoder_kernel(
                         nc.scalar.copy(out=o, in_=a)
 
         def prep_wres(j):
-            wg = work.tile([P, HALF, T], BF16, name="wresg", align_bytes=64)
-            interleave(IL_WRES[j], wg[:], wres_sb[:, :, j * HALF : (j + 1) * HALF])
+            wg = work.tile([P, HALF, T], BF16, name="wresg", align_bytes=64, bufs=1)
+            interleave(IL_WRES[j], wg[:], wres_sb[:, :, j * HALF : (j + 1) * HALF], f"r{j}")
             later[f"r{j}"] = lambda: quantize(wres_q[j], wg[:].rearrange("p n t -> p (n t)"))
 
         blocks = [(j, p) for j in range(2) for p in range(NP)]
 
         def prep_block(b):
             j, p = blocks[b]
-            wide = work.tile([P, 2, T, HALF], BF16, name="wide", bufs=3)
-            w2g = work.tile([P, 2, HALF, T], BF16, name="w2g", align_bytes=64, bufs=3)
-            wskg = work.tile([P, HALF, T], BF16, name="wskg", align_bytes=64, bufs=3)
-            col = (p % 2) * 512 + j * HALF
+            made = {}
+
+            def get(name):
+                if name not in made:
+                    shape = {"wide": [P, 2, T, HALF], "w2g": [P, 2, HALF, T], "wskg": [P, HALF, T]}[name]
+                    made[name] = work.tile(shape, BF16, name=name, align_bytes=64, bufs=3)
+                return made[name]
+
 
             def widen(g):
                 for t in range(T):
-                    fp8 = w2_sb[g][p // 2][:, t, col : col + HALF].bitcast(E4M3)
+                    fp8 = w2_sb[g][p][:, t, j * HALF : (j + 1) * HALF].bitcast(E4M3)
                     sc = scale_sb[:, g, t : t + 1]
                     if WIDEN[b][g][t] == "s":
-                        nc.scalar.activation(out=wide[:, g, t, :], in_=fp8, func=ACT.Copy, scale=sc)
+                        nc.scalar.activation(out=get("wide")[:, g, t, :], in_=fp8, func=ACT.Copy, scale=sc)
                     else:
-                        nc.vector.tensor_scalar(out=wide[:, g, t, :], in0=fp8, scalar1=sc, scalar2=None, op0=ALU.mult)
+                        nc.vector.tensor_scalar(out=get("wide")[:, g, t, :], in0=fp8, scalar1=sc, scalar2=None, op0=ALU.mult)
 
             return {
                 "n0": lambda: widen(0),
                 "n1": lambda: widen(1),
-                "k": lambda: interleave(IL_WSK[b], wskg[:], wsk_sb[p][:, :, j * HALF : (j + 1) * HALF]),
-                "i0": lambda: interleave(IL_W2[b][0], w2g[:, 0], wide[:, 0]),
-                "i1": lambda: interleave(IL_W2[b][1], w2g[:, 1], wide[:, 1]),
-                "qk": lambda: quantize(wsk_q[j][p], wskg[:].rearrange("p n t -> p (n t)")),
-                "q": lambda: quantize(w2_q[j][p], w2g[:].rearrange("p g n t -> p (g n t)")),
+                "k": lambda: interleave(IL_WSK[b], get("wskg")[:], wsk_sb[p][:, :, j * HALF : (j + 1) * HALF], f"B{b}k"),
+                "i0": lambda: interleave(IL_W2[b][0], get("w2g")[:, 0], get("wide")[:, 0], f"B{b}i0"),
+                "i1": lambda: interleave(IL_W2[b][1], get("w2g")[:, 1], get("wide")[:, 1], f"B{b}i1"),
+                "Tk": lambda: interleave("T", None, wsk_sb[p][:, :, j * HALF : (j + 1) * HALF]),
+                "Ti0": lambda: interleave("T", None, get("wide")[:, 0]),
+                "Ti1": lambda: interleave("T", None, get("wide")[:, 1]),
+                "qk": lambda: quantize(wsk_q[j][p], get("wskg")[:].rearrange("p n t -> p (n t)")),
+                "q": lambda: quantize(w2_q[j][p], get("w2g")[:].rearrange("p g n t -> p (g n t)")),
             }
 
         acc = [[keep.tile([P, 2, HALF], F32, name=f"acc{j}_{i}") for i in range(PAIRS)] for j in range(2)]
@@ -231,103 +262,124 @@ def tile_tideresidualencodertemporaldecoder_kernel(
                 mm(bank[:, c, :], x_q[i], c * P, wsk_q[j][p], 0, HALF, True, False)
                 mm(bank[:, c, :], h_q[i][0], c * P, w2_q[j][p], 0, HALF, False, False)
                 mm(bank[:, c, :], h_q[i][1], c * P, w2_q[j][p], HALF, HALF, False, True)
-            extra = None
-            if p == 0:
-                extra = psum.tile([P, 2, HALF], F32, name="bank")
+            return bank
+
+        def skip_product(b, i):
+            j, p = blocks[b]
+            if True:
+                extra = psum.tile([P, 2, HALF], F32, name="extra", bufs=2)
                 for c in range(2):
                     mm(extra[:, c, :], x_q[i], c * P, wres_q[j], 0, HALF, True, True)
-            elif FORM[j] == "b" and p == SF_AT[j]:
-                extra = psum.tile([P, 2, HALF], F32, name="bank")
+            return extra
+
+        def sf_group(j, i):
+            if True:
+                extra = psum.tile([P, 2, HALF], F32, name="extra", bufs=2)
                 for c in range(2):
-                    for q in range(NP):
+                    terms = [
+                        (diag[q], fut_sb[q][:, 2 * i + c, j * HALF : (j + 1) * HALF]) for q in range(NP)
+                    ] + [(ndiag[q], kept_m[j, i, q][:, c, :]) for q in PE_P2[j][i]]
+                    for n, (weights, moving) in enumerate(terms):
                         nc.tensor.matmul(
                             extra[:, c, :],
-                            lhsT=diag[q][:],
-                            rhs=fut_sb[q][:, 2 * i + c, j * HALF : (j + 1) * HALF],
-                            start=(q == 0),
-                            stop=(q == NP - 1),
+                            lhsT=weights[:],
+                            rhs=moving,
+                            start=(n == 0),
+                            stop=(n == len(terms) - 1),
                         )
-            return bank, extra
+            return extra
 
         def first_pass(b, i, bank):
             j, p = blocks[b]
-            m = work.tile([P, 2, HALF], F32, name="m", bufs=6)
-            f = fut_sb[p][:, 2 * i : 2 * i + 2, j * HALF : (j + 1) * HALF]
-            if FORM[j] == "b":
-                nc.vector.scalar_tensor_tensor(out=m[:], in0=bank[:], scalar=-1.0, in1=f, op0=ALU.mult, op1=ALU.min)
+            if p in PE_P2[j][i]:
+                m = work.tile([P, 2, HALF], F32, name="m_kept", bufs=4)
+                kept_m[j, i, p] = m
             else:
-                z = work.tile([P, 2, HALF], F32, name="z", bufs=4)
-                nc.vector.tensor_tensor(out=z[:], in0=bank[:], in1=f, op=ALU.add)
-                nc.scalar.activation(out=m[:], in_=z[:], func=ACT.Relu)
+                m = work.tile([P, 2, HALF], F32, name="m", bufs=6)
+            f = fut_sb[p][:, 2 * i : 2 * i + 2, j * HALF : (j + 1) * HALF]
+            nc.vector.scalar_tensor_tensor(out=m[:], in0=bank[:], scalar=-1.0, in1=f, op0=ALU.mult, op1=ALU.min)
             return m
 
-        def add_sf(b, i, extra):
-            j, p = blocks[b]
-            if FORM[j] == "b" and p == SF_AT[j]:
-                a = acc[j][i]
-                nc.vector.tensor_tensor(out=a[:], in0=a[:], in1=extra[:], op=ALU.add)
+        def finish(j, i):
+            left[j, i] -= 1
+            if left[j, i] == 0:
+                nc.sync.dma_start(
+                    out=out.rearrange("(q i c) (j n) -> i j q c n", c=2, i=PAIRS, j=2)[i, j], in_=acc[j][i][:]
+                )
+
+        left = {(j, i): 5 - len(PE_P2[j][i]) for j in range(2) for i in range(PAIRS)}
+
+        def add_sf(j, i, extra):
+            a = acc[j][i]
+            nc.vector.tensor_tensor(out=a[:], in0=a[:], in1=extra[:], op=ALU.add)
+            finish(j, i)
 
         def second_pass(b, i, m, extra):
             j, p = blocks[b]
             a = acc[j][i]
+            if p in PE_P2[j][i]:
+                return
             nc.vector.scalar_tensor_tensor(
                 out=a[:],
                 in0=m[:],
-                scalar=(nv_col if FORM[j] == "b" else v_col)[:, p : p + 1],
+                scalar=nv_col[:, p : p + 1],
                 in1=extra[:] if p == 0 else a[:],
                 op0=ALU.mult,
                 op1=ALU.add,
             )
-            if p == NP - 1:
-                nc.sync.dma_start(
-                    out=out.rearrange("(q i c) (j n) -> i j q c n", c=2, i=PAIRS, j=2)[i, j], in_=a[:]
-                )
+            finish(j, i)
+
+        steps = [(b, i) for b in range(len(blocks)) for i in range(PAIRS)]
+        banks, extras, ms = {}, {}, {}
+        preps = {}
+        kept = {}
+
+        def emit(k):
+            kind, n = k[0], k[1:]
+            if kind == "B":
+                b = int(n[0])
+                if b not in preps:
+                    preps[b] = prep_block(b)
+                preps[b][n[1:]]()
+            elif kind == "q":
+                later[n]()
+            elif kind == "x":
+                copy_x(int(n))
+            elif kind == "X":
+                turn_x(int(n))
+            elif kind == "w":
+                prep_w1(int(n))
+            elif kind == "r":
+                prep_wres(int(n))
+            elif kind == "h":
+                copy_h(int(n[0]), int(n[1]), int(n[2]))
+            elif kind == "H":
+                hidden(int(n[0]), int(n[1]), int(n[2]))
+            elif kind == "V":
+                spread_v()
+            elif kind == "M":
+                banks[int(n)] = multiply(*steps[int(n)])
+            elif kind == "W":
+                extras[int(n)] = skip_product(*steps[int(n)])
+            elif kind == "T":
+                if n[0] == "r":
+                    j = int(n[1])
+                    spread_banks[n] = interleave("T", None, wres_sb[:, :, j * HALF : (j + 1) * HALF])
+                else:
+                    b = int(n[1])
+                    if b not in preps:
+                        preps[b] = prep_block(b)
+                    spread_banks[n] = preps[b]["T" + n[2:]]()
+            elif kind == "P":
+                ms[int(n)] = first_pass(*steps[int(n)], banks[int(n)])
+            elif kind == "S":
+                second_pass(*steps[int(n)], ms[int(n)], extras.get(int(n)))
+            elif kind == "F":
+                kept[n] = sf_group(int(n[0]), int(n[1]))
+            elif kind == "A":
+                add_sf(int(n[0]), int(n[1]), kept[n])
 
         if MANUAL:
             ctx.enter_context(tc.manual_schedule())
-        todo = {"V": spread_v}
-        for i in range(PAIRS):
-            todo[f"x{i}"] = lambda i=i: prep_x(i)
-            for g in range(2):
-                todo[f"h{i}{g}"] = lambda i=i, g=g: hidden(i, g)
-        for g in range(2):
-            todo[f"w{g}"] = lambda g=g: prep_w1(g)
-            todo[f"r{g}"] = lambda g=g: prep_wres(g)
-        preps = {}
-
-        def emit(k):
-            if k[0] == "B":
-                b = int(k[1])
-                if b not in preps:
-                    preps[b] = prep_block(b)
-                preps[b][k[2:]]()
-            elif k[0] == "q":
-                later[k[1:]]()
-            else:
-                todo[k]()
-
-        for k in HEAD.split():
+        for k in ORDER.split():
             emit(k)
-        fill = {}
-        for k, at in FILL.items():
-            fill.setdefault(at, []).append(k)
-        for b in range(2, len(blocks)):
-            for k, at in OFFS.items():
-                fill.setdefault(4 * b + at, []).append(f"B{b}{k}")
-        pending = []
-        for st in range(4 * len(blocks)):
-            b, i = divmod(st, PAIRS)
-            bank, extra = multiply(b, i)
-            for k in fill.get(st, []):
-                if k[2:] not in ("q", "qk") and k[0] != "q":
-                    emit(k)
-            m = first_pass(b, i, bank)
-            for k in fill.get(st, []):
-                if k[2:] in ("q", "qk") or k[0] == "q":
-                    emit(k)
-            if len(pending) >= LAG:
-                second_pass(*pending.pop(0))
-            add_sf(b, i, extra)
-            pending.append((b, i, m, extra))
-        for q in pending:
-            second_pass(*q)

@@ -19,15 +19,17 @@ P = 128
 T = 4
 HALF = 256
 PAIRS = N // (2 * P)
-IL_WSK = ["v","s","s","s","s","s","s","s"]
-IL_W2 = [["s","s"],["s","s"],["s","s"],["s","v"],["v","v"],["s","s"],["s","s"],["s","s"]]
-IL_WRES = ["s","v"]
-H_ENG = [[["s","s"],["s","s"]],[["s","s"],["s","s"]],[["s","v"],["s","s"]],[["v","s"],["s","s"]]]
-X_ENG = ["s","v","s","s"]
-WIDEN = [["ssss","ssss"],["ssss","vvvv"],["ssss","ssss"],["ssss","ssss"],["vvvv","vvvv"],["ssss","ssss"],["ssss","ssss"],["ssss","ssss"]]
-PE_P2 = [[[],[1],[1],[]],[[2],[],[1],[2]]]
-LOADS = "m00 w11 m10 x3 x1 w10 r x2 k0 f0 x0 g1 m11 k1 m02 m01 f1 k2 m12 g0"
-ORDER = "B4n0 B0n0 B4i0 B0i0 w1 B0n1 B4n1 X3 qw1 X1 x3 V B4i1 B0i1 qx3 B4q H310 H311 x1 h310 B0q h311 qx1 r0 X2 qh31 w0 H110 H111 x2 B4k qr0 qw0 W1 W3 qx2 H100 r1 h110 H200 H201 h200 B4qk H101 h201 H300 h111 B0k h100 H301 h300 h101 X0 B0qk h301 H210 qh10 qh11 x0 H211 qh30 M1 h210 qr1 qx0 h211 qh20 H000 P1 H001 h000 H010 B1n1 H011 h001 M3 qh21 h010 S1 M2 h011 qh00 P3 B1i1 W0 qh01 M17 P2 S3 B1k M0 P17 W2 P0 M16 B1n0 B1qk S0 M18 B3n0 S2 W16 P16 W17 M19 B1i0 P18 S16 P19 B3i0 F03 S17 B1q W18 B3k S18 M4 A03 B2n1 M5 B3qk P4 M6 P5 B3n1 S4 M7 P6 B5n0 F00 B3i1 P7 B5k F11 B3q S7 B6n0 M12 B5qk A00 M13 B5n1 P12 M14 A11 B5i0 P13 M15 P14 W19 S12 B5i1 F02 S13 S14 B6k B5q S19 M20 B6n1 B6qk P15 M21 B6i0 P20 M22 S15 P21 B6i1 M23 P22 F01 S20 B7k B6q P23 B2k B7qk S21 M24 S23 B2n0 M25 P24 B2qk M26 B2i1 P25 A02 M27 B2i0 P26 F10 P27 S25 B7n0 B2q S26 B7n1 M8 A10 A01 M9 B7i0 P8 M10 P9 B7i1 S8 M11 P10 F12 B7q P11 S9 S10 M28 S11 M29 A12 P28 M30 P29 M31 S28 P30 F13 P31 S29 S30 S31 A13"
+FORM = [[0,0,0,0],[0,0,0,0]]
+IL_W1 = ["v","v","s","v"]
+IL_WSK = ["pe","v","pe","pe","v","s","s","s"]
+IL_W2 = [["pe","v"],["s","s"],["s","s"],["s","pe"],["v","s"],["s","s"],["s","s"],["s","s"]]
+IL_WRES = ["v","s"]
+H_ENG = [[["s","v"],["s","s"]],[["s","s"],["v","s"]],[["s","s"],["s","v"]],[["s","s"],["s","s"]]]
+X_ENG = ["s","s","s","s"]
+WIDEN = [["ssss","vvvv"],["ssss","ssss"],["ssss","ssss"],["ssss","ssss"],["vvvv","ssss"],["ssss","ssss"],["ssss","ssss"],["ssss","ssss"]]
+PE_P2 = [[[1],[1],[],[]],[[2],[],[1],[2]]]
+LOADS = "m10 x0 m00 w10 w1b x2 x1 a0 k0 x3 g1 r m11 a1 m01 k1 g0"
+ORDER = "B0n1 B4n1 X0 B0i1 B4i1 B4n0 B4i0 x0 V w2 B0n0 B4q qx0 w4 TB0i0 w3 X2 w5 B0i0 X1 qw0 x2 qw1 H000 x1 H001 qx2 H010 h000 B0q H200 h010 H201 h001 H210 h200 qx1 H211 qh00 H011 h201 h211 D H110 TB0k h210 h110 H111 h011 B4k X3 B0k qh01 H100 x3 B4qk H101 qh21 M16 h111 B0qk qx3 h100 qh11 H310 P16 H311 h101 H300 qh20 h310 H301 qh10 M0 r0 h311 h300 M1 qh31 qr0 h301 P0 W0 r1 W1 qh30 M2 S0 P1 W2 B1n1 M3 qr1 S1 M17 B2n1 P2 P3 F02 B1i1 S2 P17 W3 M18 B1n0 A02 S3 W16 M19 S16 B3n1 P18 W17 F03 S17 B1i0 P19 TB3i1 B1k B3n0 TB2k B1q TB3k B1qk B3i1 W18 A03 M4 B2k S18 B3k F11 P4 B3i0 B3qk B2qk M5 A11 B5k B3q M6 P5 M7 B5n1 P6 B5qk M12 S6 B5n0 P7 M13 P12 B5i1 M14 S7 S12 M15 B5i0 P13 W19 P14 F00 B6k S13 B5q S14 B7k M20 B6qk S19 B2n0 M21 B7qk P15 M22 P20 B2i1 S15 M23 S20 B2i0 F01 P21 P22 B6n1 B2q S21 B6n0 M8 P23 A00 M9 B6i1 P8 M10 S23 S8 B6i0 M11 P9 F12 P10 B7n1 B6q S9 B7n0 S10 M24 P11 B7i1 A01 M25 S11 B7i0 M26 P24 P25 F10 P26 B7q S25 S26 M27 A10 M28 P27 A12 M29 P28 M30 P29 S28 M31 S29 F13 P30 P31 S30 S31 A13"
 MANUAL = True
 
 
@@ -41,41 +43,35 @@ def tile_tideresidualencodertemporaldecoder_kernel(
         psum = ctx.enter_context(tc.psum_pool(name="psum", bufs=6))
 
         x_sb = [keep.tile([P, 2, L], BF16, name=f"x_sb{i}") for i in range(PAIRS)]
-        w1_sb = [keep.tile([P, T, 512], BF16, name=f"w1_sb{g}") for g in range(2)]
-        wsk_lo = [keep.tile([P, T, 512], BF16, name=f"wsk_sb{p}") for p in range(2)]
-        wsk_hi = keep.tile([P, T, 1024], BF16, name="wsk_hi")
-        wsk_sb = [wsk_lo[0][:], wsk_lo[1][:], wsk_hi[:, :, 0:512], wsk_hi[:, :, 512:1024]]
-        w2_lo = [[keep.tile([P, T, 512], U8, name=f"w2_lo{g}_{p}") for p in range(2)] for g in range(2)]
-        w2_hi = [keep.tile([P, T, 1024], U8, name=f"w2_hi{g}") for g in range(2)]
-        w2_sb = [[w2_lo[g][0][:], w2_lo[g][1][:], w2_hi[g][:, :, 0:512], w2_hi[g][:, :, 512:1024]] for g in range(2)]
-        wres_sb = keep.tile([P, T, 512], BF16, name="wres_sb")
-        fut_lo = [keep.tile([P, 8, 512], BF16, name=f"fut_lo{p}") for p in range(2)]
-        fut_hi = keep.tile([P, 8, 2, 512], BF16, name="fut_hi")
-        fut_sb = [fut_lo[0][:], fut_lo[1][:], fut_hi[:, :, 0, :], fut_hi[:, :, 1, :]]
+        w1_sb = keep.tile([P, T, F], BF16, name="w1_sb")
+        wsk_sb = keep.tile([P, T, NP * H], BF16, name="wsk_sb")
+        w2_sb = [keep.tile([P, T, NP * H], U8, name=f"w2_sb{g}") for g in range(2)]
+        wres_sb = keep.tile([P, T, H], BF16, name="wres_sb")
+        fut_sb = keep.tile([P, 8, NP, H], BF16, name="fut_sb")
         scale_sb = keep.tile([P, 2, T], F32, name="scale_sb")
         vp_sb = keep.tile([P, NP], BF16, name="vp_sb")
         nc.vector.memset(vp_sb[:], 0.0)
 
         x_v = x.rearrange("(q i c) k -> i q c k", c=2, i=PAIRS)
-        w1_v = w1.rearrange("(p j) (g f) -> g p j f", j=T, g=2)
-        wsk_v = wsk.rearrange("(p j) (b n) -> b p j n", j=T, b=NP)
-        w2_v = w2_bytes.rearrange("(g p t) (b n) -> g b p t n", g=2, t=T, b=4)
-        w2_hv = w2_bytes.rearrange("(g p t) (b n) -> g b p t n", g=2, t=T, b=2)
-        fut_v = fut.rearrange("(q c) b n -> b q c n", q=P)
-        fut_hv = fut.rearrange("(q c) (h b) n -> h q c b n", q=P, h=2)
-        wsk_hv = wsk.rearrange("(p j) (h n) -> h p j n", j=T, h=2)
+        w1_v = w1.rearrange("(p j) f -> p j f", j=T)
+        wsk_v = wsk.rearrange("(p j) n -> p j n", j=T)
+        w2_v = w2_bytes.rearrange("(g p t) n -> g p t n", g=2, t=T)
+        fut_v = fut.rearrange("(q c) b n -> q c b n", q=P)
 
         def load(dst, src):
             nc.sync.dma_start(out=dst, in_=src)
 
         pieces = {f"x{i}": (x_sb[i][:], x_v[i]) for i in range(PAIRS)}
-        pieces.update({f"w1{g}": (w1_sb[g][:], w1_v[g]) for g in range(2)})
-        pieces.update({f"k{p}": (wsk_lo[p][:], wsk_v[p]) for p in range(2)})
-        pieces.update({f"f{p}": (fut_lo[p][:], fut_v[p]) for p in range(2)})
-        pieces.update({f"g{h}": (fut_hi[:, 4 * h : 4 * h + 4], fut_hv[1][:, 4 * h : 4 * h + 4]) for h in range(2)})
-        pieces.update({f"m{g}{b}": (w2_lo[g][b][:], w2_v[g, b]) for g in range(2) for b in range(2)})
-        pieces.update({f"m{g}2": (w2_hi[g][:], w2_hv[g, 1]) for g in range(2)})
-        pieces["k2"] = (wsk_hi[:], wsk_hv[1])
+        pieces["w10"] = (w1_sb[:, :, 0:HALF], w1_v[:, :, 0:HALF])
+        pieces["w1b"] = (w1_sb[:, :, HALF:F], w1_v[:, :, HALF:F])
+        pieces["k0"] = (wsk_sb[:, :, 0:H], wsk_v[:, :, 0:H])
+        pieces["k1"] = (wsk_sb[:, :, H : NP * H], wsk_v[:, :, H : NP * H])
+        for g in range(2):
+            pieces[f"m{g}0"] = (w2_sb[g][:, :, 0:H], w2_v[g][:, :, 0:H])
+            pieces[f"m{g}1"] = (w2_sb[g][:, :, H : NP * H], w2_v[g][:, :, H : NP * H])
+        for h in range(2):
+            pieces[f"a{h}"] = (fut_sb[:, 4 * h : 4 * h + 4, 0:2, :], fut_v[:, 4 * h : 4 * h + 4, 0:2, :])
+            pieces[f"g{h}"] = (fut_sb[:, 4 * h : 4 * h + 4, 2:4, :], fut_v[:, 4 * h : 4 * h + 4, 2:4, :])
         pieces["r"] = (wres_sb[:], wres.rearrange("(p j) n -> p j n", j=T))
         nc.scalar.dma_start(out=scale_sb[:], in_=w2_scale.rearrange("(g p t) o -> p g (t o)", g=2, t=T))
         nc.scalar.dma_start(out=vp_sb[0:1, :], in_=vp.rearrange("(o n) -> o n", o=1))
@@ -102,6 +98,8 @@ def tile_tideresidualencodertemporaldecoder_kernel(
             nc.tensor.matmul(bank[:], lhsT=ones[:], rhs=vp_sb[:], start=True, stop=True)
             nc.scalar.copy(out=v_col[:], in_=bank[:])
             nc.scalar.activation(out=nv_col[:], in_=v_col[:], func=ACT.Copy, scale=-1.0)
+
+        def build_diagonals():
             for p in ndiag:
                 nc.gpsimd.tensor_scalar(
                     out=ndiag[p][:], in0=ident_f32[:], scalar1=nv_col[:, p : p + 1], scalar2=0.0, op0=ALU.mult, op1=ALU.add
@@ -158,9 +156,22 @@ def tile_tideresidualencodertemporaldecoder_kernel(
             )
             later[f"x{i}"] = lambda: quantize(x_q[i], xg[:].rearrange("p c n t -> p (c n t)"))
 
-        def prep_w1(g):
-            wg = work.tile([P, T, P, T], BF16, name="w1g", align_bytes=64)
-            nc.vector.tensor_copy(out=wg[:], in_=w1_sb[g][:].rearrange("p j (m t) -> p t m j", t=T))
+        w1_tiles = {}
+
+        def prep_w1(g, m0, m1, piece=0):
+            if g not in w1_tiles:
+                w1_tiles[g] = work.tile([P, T, P, T], BF16, name="w1g", align_bytes=64)
+            wg = w1_tiles[g]
+            half = m0 // 64
+            o = wg[:, :, m0:m1, :]
+            a = w1_sb[:, :, 512 * g + T * m0 : 512 * g + T * m1].rearrange("p j (m t) -> p t m j", t=T)
+            if IL_W1[2 * g + half] == "v":
+                nc.vector.tensor_copy(out=o, in_=a)
+            elif IL_W1[2 * g + half] == "s":
+                nc.scalar.copy(out=o, in_=a)
+            else:
+                for u0, u1 in [((0, 22), (22, 43), (43, 64))[piece]]:
+                    nc.gpsimd.tensor_scalar(out=o[:, :, u0:u1], in0=a[:, :, u0:u1], scalar1=1.0, scalar2=0.0, op0=ALU.mult, op1=ALU.add)
             later[f"w{g}"] = lambda: quantize(w1_q[g], wg[:].rearrange("p t m j -> p (t m j)"))
 
         def hidden(i, g, c):
@@ -185,7 +196,7 @@ def tile_tideresidualencodertemporaldecoder_kernel(
 
         spread_banks = {}
 
-        def interleave(engine, dst, src, key=None):
+        def interleave(engine, dst, src, key=None, piece=0):
             if engine == "T":
                 bank = psum.tile([P, HALF, T], BF16, name="bank")
                 for n0 in range(0, HALF, P):
@@ -201,20 +212,24 @@ def tile_tideresidualencodertemporaldecoder_kernel(
                 nc.scalar.copy(out=dst, in_=spread_banks[key][:])
             else:
                 cuts = [0, 88, 172, HALF] if engine == "g" else [0, HALF]
-                for n0, n1 in zip(cuts, cuts[1:]):
+                for n0, n1 in [(cuts[piece], cuts[piece + 1])]:
                     part = slice(n0, n1)
                     o = dst[:, part].rearrange("p (c i) j -> p c j i", i=4)
                     a = src[:, :, part].rearrange("p j (c i) -> p c j i", i=4)
                     if engine == "g":
-                        nc.gpsimd.tensor_scalar(out=o, in0=a, scalar1=1.0, scalar2=0.0, op0=ALU.mult, op1=ALU.add)
+                        nc.gpsimd.tensor_scalar(out=dst[:, part], in0=src[:, :, part].rearrange("p j n -> p n j"), scalar1=1.0, scalar2=0.0, op0=ALU.mult, op1=ALU.add)
                     elif engine == "v":
                         nc.vector.tensor_copy(out=o, in_=a)
                     else:
                         nc.scalar.copy(out=o, in_=a)
 
-        def prep_wres(j):
-            wg = work.tile([P, HALF, T], BF16, name="wresg", align_bytes=64, bufs=1)
-            interleave(IL_WRES[j], wg[:], wres_sb[:, :, j * HALF : (j + 1) * HALF], f"r{j}")
+        wres_tiles = {}
+
+        def prep_wres(j, piece=0):
+            if j not in wres_tiles:
+                wres_tiles[j] = work.tile([P, HALF, T], BF16, name="wresg", align_bytes=64, bufs=1)
+            wg = wres_tiles[j]
+            interleave(IL_WRES[j], wg[:], wres_sb[:, :, j * HALF : (j + 1) * HALF], f"r{j}", piece)
             later[f"r{j}"] = lambda: quantize(wres_q[j], wg[:].rearrange("p n t -> p (n t)"))
 
         blocks = [(j, p) for j in range(2) for p in range(NP)]
@@ -232,7 +247,7 @@ def tile_tideresidualencodertemporaldecoder_kernel(
 
             def widen(g):
                 for t in range(T):
-                    fp8 = w2_sb[g][p][:, t, j * HALF : (j + 1) * HALF].bitcast(E4M3)
+                    fp8 = w2_sb[g][:, t, p * H + j * HALF : p * H + (j + 1) * HALF].bitcast(E4M3)
                     sc = scale_sb[:, g, t : t + 1]
                     if WIDEN[b][g][t] == "s":
                         nc.scalar.activation(out=get("wide")[:, g, t, :], in_=fp8, func=ACT.Copy, scale=sc)
@@ -242,10 +257,10 @@ def tile_tideresidualencodertemporaldecoder_kernel(
             return {
                 "n0": lambda: widen(0),
                 "n1": lambda: widen(1),
-                "k": lambda: interleave(IL_WSK[b], get("wskg")[:], wsk_sb[p][:, :, j * HALF : (j + 1) * HALF], f"B{b}k"),
-                "i0": lambda: interleave(IL_W2[b][0], get("w2g")[:, 0], get("wide")[:, 0], f"B{b}i0"),
-                "i1": lambda: interleave(IL_W2[b][1], get("w2g")[:, 1], get("wide")[:, 1], f"B{b}i1"),
-                "Tk": lambda: interleave("T", None, wsk_sb[p][:, :, j * HALF : (j + 1) * HALF]),
+                "k": lambda piece=0: interleave(IL_WSK[b], get("wskg")[:], wsk_sb[:, :, p * H + j * HALF : p * H + (j + 1) * HALF], f"B{b}k", piece),
+                "i0": lambda piece=0: interleave(IL_W2[b][0], get("w2g")[:, 0], get("wide")[:, 0], f"B{b}i0", piece),
+                "i1": lambda piece=0: interleave(IL_W2[b][1], get("w2g")[:, 1], get("wide")[:, 1], f"B{b}i1", piece),
+                "Tk": lambda: interleave("T", None, wsk_sb[:, :, p * H + j * HALF : p * H + (j + 1) * HALF]),
                 "Ti0": lambda: interleave("T", None, get("wide")[:, 0]),
                 "Ti1": lambda: interleave("T", None, get("wide")[:, 1]),
                 "qk": lambda: quantize(wsk_q[j][p], get("wskg")[:].rearrange("p n t -> p (n t)")),
@@ -277,7 +292,7 @@ def tile_tideresidualencodertemporaldecoder_kernel(
                 extra = psum.tile([P, 2, HALF], F32, name="extra", bufs=2)
                 for c in range(2):
                     terms = [
-                        (diag[q], fut_sb[q][:, 2 * i + c, j * HALF : (j + 1) * HALF]) for q in range(NP)
+                        (diag[q], fut_sb[:, 2 * i + c, q, j * HALF : (j + 1) * HALF]) for q in range(NP)
                     ] + [(ndiag[q], kept_m[j, i, q][:, c, :]) for q in PE_P2[j][i]]
                     for n, (weights, moving) in enumerate(terms):
                         nc.tensor.matmul(
@@ -296,8 +311,11 @@ def tile_tideresidualencodertemporaldecoder_kernel(
                 kept_m[j, i, p] = m
             else:
                 m = work.tile([P, 2, HALF], F32, name="m", bufs=6)
-            f = fut_sb[p][:, 2 * i : 2 * i + 2, j * HALF : (j + 1) * HALF]
-            nc.vector.scalar_tensor_tensor(out=m[:], in0=bank[:], scalar=-1.0, in1=f, op0=ALU.mult, op1=ALU.min)
+            f = fut_sb[:, 2 * i : 2 * i + 2, p, j * HALF : (j + 1) * HALF]
+            if FORM[j][i]:
+                nc.vector.tensor_tensor(out=m[:], in0=bank[:], in1=f, op=ALU.add)
+            else:
+                nc.vector.scalar_tensor_tensor(out=m[:], in0=bank[:], scalar=-1.0, in1=f, op0=ALU.mult, op1=ALU.min)
             return m
 
         def finish(j, i):
@@ -307,7 +325,7 @@ def tile_tideresidualencodertemporaldecoder_kernel(
                     out=out.rearrange("(q i c) (j n) -> i j q c n", c=2, i=PAIRS, j=2)[i, j], in_=acc[j][i][:]
                 )
 
-        left = {(j, i): 5 - len(PE_P2[j][i]) for j in range(2) for i in range(PAIRS)}
+        left = {(j, i): 4 if FORM[j][i] else 5 - len(PE_P2[j][i]) for j in range(2) for i in range(PAIRS)}
 
         def add_sf(j, i, extra):
             a = acc[j][i]
@@ -322,7 +340,7 @@ def tile_tideresidualencodertemporaldecoder_kernel(
             nc.vector.scalar_tensor_tensor(
                 out=a[:],
                 in0=m[:],
-                scalar=nv_col[:, p : p + 1],
+                scalar=(v_col if FORM[j][i] else nv_col)[:, p : p + 1],
                 in1=extra[:] if p == 0 else a[:],
                 op0=ALU.mult,
                 op1=ALU.add,
@@ -336,6 +354,19 @@ def tile_tideresidualencodertemporaldecoder_kernel(
 
         def emit(k):
             kind, n = k[0], k[1:]
+            if kind == "g":
+                piece = int(n[0])
+                if n[1] == "B":
+                    b = int(n[2])
+                    if b not in preps:
+                        preps[b] = prep_block(b)
+                    preps[b][n[3:]](piece)
+                elif n[1] == "r":
+                    prep_wres(int(n[2]), piece)
+                else:
+                    q = int(n[2])
+                    prep_w1((q - 2) // 2, 64 * (q % 2), 64 * (q % 2) + 64, piece)
+                return
             if kind == "B":
                 b = int(n[0])
                 if b not in preps:
@@ -348,7 +379,7 @@ def tile_tideresidualencodertemporaldecoder_kernel(
             elif kind == "X":
                 turn_x(int(n))
             elif kind == "w":
-                prep_w1(int(n))
+                prep_w1((int(n) - 2) // 2, 64 * (int(n) % 2), 64 * (int(n) % 2) + 64)
             elif kind == "r":
                 prep_wres(int(n))
             elif kind == "h":
@@ -357,6 +388,8 @@ def tile_tideresidualencodertemporaldecoder_kernel(
                 hidden(int(n[0]), int(n[1]), int(n[2]))
             elif kind == "V":
                 spread_v()
+            elif kind == "D":
+                build_diagonals()
             elif kind == "M":
                 banks[int(n)] = multiply(*steps[int(n)])
             elif kind == "W":
@@ -372,6 +405,8 @@ def tile_tideresidualencodertemporaldecoder_kernel(
                     spread_banks[n] = preps[b]["T" + n[2:]]()
             elif kind == "P":
                 ms[int(n)] = first_pass(*steps[int(n)], banks[int(n)])
+            elif kind == "R":
+                nc.scalar.activation(out=ms[int(n)][:], in_=ms[int(n)][:], func=ACT.Relu)
             elif kind == "S":
                 second_pass(*steps[int(n)], ms[int(n)], extras.get(int(n)))
             elif kind == "F":

@@ -20,16 +20,16 @@ T = 4
 HALF = 256
 PAIRS = N // (2 * P)
 FORM = [[0,0,0,0],[0,0,0,0]]
-IL_W1 = ["v","v","s","v"]
-IL_WSK = ["pe","v","pe","pe","v","s","s","s"]
-IL_W2 = [["pe","v"],["s","s"],["s","s"],["s","pe"],["v","s"],["s","s"],["s","s"],["s","s"]]
+IL_W1 = ["s","v","s","v"]
+IL_WSK = ["v","v","s","s","s","s","s","s"]
+IL_W2 = [["v","v"],["s","s"],["s","s"],["s","s"],["v","s"],["s","s"],["s","s"],["s","s"]]
 IL_WRES = ["v","s"]
-H_ENG = [[["s","v"],["s","s"]],[["s","s"],["v","s"]],[["s","s"],["s","v"]],[["s","s"],["s","s"]]]
-X_ENG = ["s","s","s","s"]
-WIDEN = [["ssss","vvvv"],["ssss","ssss"],["ssss","ssss"],["ssss","ssss"],["vvvv","ssss"],["ssss","ssss"],["ssss","ssss"],["ssss","ssss"]]
-PE_P2 = [[[1],[1],[],[]],[[2],[],[1],[2]]]
-LOADS = "m10 x0 m00 w10 w1b x2 x1 a0 k0 x3 g1 r m11 a1 m01 k1 g0"
-ORDER = "B0n1 B4n1 X0 B0i1 B4i1 B4n0 B4i0 x0 V w2 B0n0 B4q qx0 w4 TB0i0 w3 X2 w5 B0i0 X1 qw0 x2 qw1 H000 x1 H001 qx2 H010 h000 B0q H200 h010 H201 h001 H210 h200 qx1 H211 qh00 H011 h201 h211 D H110 TB0k h210 h110 H111 h011 B4k X3 B0k qh01 H100 x3 B4qk H101 qh21 M16 h111 B0qk qx3 h100 qh11 H310 P16 H311 h101 H300 qh20 h310 H301 qh10 M0 r0 h311 h300 M1 qh31 qr0 h301 P0 W0 r1 W1 qh30 M2 S0 P1 W2 B1n1 M3 qr1 S1 M17 B2n1 P2 P3 F02 B1i1 S2 P17 W3 M18 B1n0 A02 S3 W16 M19 S16 B3n1 P18 W17 F03 S17 B1i0 P19 TB3i1 B1k B3n0 TB2k B1q TB3k B1qk B3i1 W18 A03 M4 B2k S18 B3k F11 P4 B3i0 B3qk B2qk M5 A11 B5k B3q M6 P5 M7 B5n1 P6 B5qk M12 S6 B5n0 P7 M13 P12 B5i1 M14 S7 S12 M15 B5i0 P13 W19 P14 F00 B6k S13 B5q S14 B7k M20 B6qk S19 B2n0 M21 B7qk P15 M22 P20 B2i1 S15 M23 S20 B2i0 F01 P21 P22 B6n1 B2q S21 B6n0 M8 P23 A00 M9 B6i1 P8 M10 S23 S8 B6i0 M11 P9 F12 P10 B7n1 B6q S9 B7n0 S10 M24 P11 B7i1 A01 M25 S11 B7i0 M26 P24 P25 F10 P26 B7q S25 S26 M27 A10 M28 P27 A12 M29 P28 M30 P29 S28 M31 S29 F13 P30 P31 S30 S31 A13"
+H_ENG = [[["s","s"],["s","s"]],[["v","v"],["s","s"]],[["s","s"],["s","s"]],[["s","s"],["s","s"]]]
+X_ENG = ["s","s","s","v"]
+WIDEN = [["vvvv","vvvv"],["ssss","vvvv"],["ssss","ssss"],["ssss","ssss"],["vvvv","ssss"],["ssss","ssss"],["ssss","ssss"],["ssss","ssss"]]
+PE_P2 = [[[1],[2],[],[1]],[[2],[],[],[2]]]
+LOADS = "m10 m00 w10 x2 x0 w1b x1 k0 r a0 x3 g1 m11 a1 m01 k1 g0"
+ORDER = "B0n1 B4n1 B0i1 B4i1 B0n0 B4n0 X2 w2 B0i0 X0 B4i0 x2 V B0q x0 B4q w4 w3 X1 qx2 qw0 x1 qx0 H200 B4k qx1 H201 B0k H000 H001 w5 H100 h200 H101 B4qk h201 qw1 h000 qh20 H010 h100 D h001 H011 H210 h101 h010 H211 H110 qh00 h011 X3 qh10 h210 B0qk H111 qh01 h211 x3 M0 h110 r0 M16 h111 qx3 qr0 H300 qh11 r1 H301 P0 H310 qh21 H311 P16 W0 h300 M1 B1n1 h301 W1 S0 B1i1 M2 P1 W2 qh30 h310 M17 S1 h311 P2 F02 B2n1 P17 qh31 M18 S2 B3n1 qr1 M3 A02 B1n0 P18 W3 W16 P3 M19 S16 B3i1 S3 P19 W17 B1i0 W18 S17 S18 W19 B3n0 S19 F12 B1k B3k F11 B1q B1qk B3i0 A12 M4 B3qk A11 M5 B5n1 B3q M6 P4 B5n0 P5 M7 P6 B5i1 M12 S5 S6 M13 B5i0 P7 M14 P12 P13 B2k F03 B5q S12 B5k S13 P14 M15 B6k B5qk S14 M20 P15 B2n0 M21 B6qk S15 F00 B2i1 P20 P21 B2i0 S20 S21 M22 B2qk B6n1 B2q M23 P22 B6n0 A03 M8 S22 M9 B6i1 P8 P23 M10 S8 B6i0 M11 P9 P10 F01 B7n1 B6q S10 B7n0 P11 S23 M24 B7i1 S11 M25 P24 B7i0 A00 M26 P25 F10 B7k P26 B7q S25 B7qk M27 S26 A10 M28 P27 M29 A01 P28 M30 P29 M31 S28 S29 F13 P30 P31 S30 S31 A13"
 MANUAL = True
 
 
@@ -43,11 +43,14 @@ def tile_tideresidualencodertemporaldecoder_kernel(
         psum = ctx.enter_context(tc.psum_pool(name="psum", bufs=6))
 
         x_sb = [keep.tile([P, 2, L], BF16, name=f"x_sb{i}") for i in range(PAIRS)]
-        w1_sb = keep.tile([P, T, F], BF16, name="w1_sb")
-        wsk_sb = keep.tile([P, T, NP * H], BF16, name="wsk_sb")
-        w2_sb = [keep.tile([P, T, NP * H], U8, name=f"w2_sb{g}") for g in range(2)]
+        w1_lo = keep.tile([P, T, HALF], BF16, name="w1_lo")
+        w1_hi = keep.tile([P, T, F - HALF], BF16, name="w1_hi")
+        wsk_lo = keep.tile([P, T, H], BF16, name="wsk_lo")
+        wsk_hi = keep.tile([P, T, 3 * H], BF16, name="wsk_hi")
+        w2_lo = [keep.tile([P, T, H], U8, name=f"w2_lo{g}") for g in range(2)]
+        w2_hi = [keep.tile([P, T, 3 * H], U8, name=f"w2_hi{g}") for g in range(2)]
         wres_sb = keep.tile([P, T, H], BF16, name="wres_sb")
-        fut_sb = keep.tile([P, 8, NP, H], BF16, name="fut_sb")
+        fut_sb = [[keep.tile([P, 4, 2, H], BF16, name=f"fut_sb{h}{b}") for b in range(2)] for h in range(2)]
         scale_sb = keep.tile([P, 2, T], F32, name="scale_sb")
         vp_sb = keep.tile([P, NP], BF16, name="vp_sb")
         nc.vector.memset(vp_sb[:], 0.0)
@@ -61,17 +64,25 @@ def tile_tideresidualencodertemporaldecoder_kernel(
         def load(dst, src):
             nc.sync.dma_start(out=dst, in_=src)
 
+        def wsk_cols(p, j):
+            c0 = p * H + j * HALF
+            return wsk_lo[:, :, c0 : c0 + HALF] if p == 0 else wsk_hi[:, :, c0 - H : c0 - H + HALF]
+
+        def w2_cols(g, t, p, j):
+            c0 = p * H + j * HALF
+            return w2_lo[g][:, t, c0 : c0 + HALF] if p == 0 else w2_hi[g][:, t, c0 - H : c0 - H + HALF]
+
         pieces = {f"x{i}": (x_sb[i][:], x_v[i]) for i in range(PAIRS)}
-        pieces["w10"] = (w1_sb[:, :, 0:HALF], w1_v[:, :, 0:HALF])
-        pieces["w1b"] = (w1_sb[:, :, HALF:F], w1_v[:, :, HALF:F])
-        pieces["k0"] = (wsk_sb[:, :, 0:H], wsk_v[:, :, 0:H])
-        pieces["k1"] = (wsk_sb[:, :, H : NP * H], wsk_v[:, :, H : NP * H])
+        pieces["w10"] = (w1_lo[:], w1_v[:, :, 0:HALF])
+        pieces["w1b"] = (w1_hi[:], w1_v[:, :, HALF:F])
+        pieces["k0"] = (wsk_lo[:], wsk_v[:, :, 0:H])
+        pieces["k1"] = (wsk_hi[:], wsk_v[:, :, H : NP * H])
         for g in range(2):
-            pieces[f"m{g}0"] = (w2_sb[g][:, :, 0:H], w2_v[g][:, :, 0:H])
-            pieces[f"m{g}1"] = (w2_sb[g][:, :, H : NP * H], w2_v[g][:, :, H : NP * H])
+            pieces[f"m{g}0"] = (w2_lo[g][:], w2_v[g][:, :, 0:H])
+            pieces[f"m{g}1"] = (w2_hi[g][:], w2_v[g][:, :, H : NP * H])
         for h in range(2):
-            pieces[f"a{h}"] = (fut_sb[:, 4 * h : 4 * h + 4, 0:2, :], fut_v[:, 4 * h : 4 * h + 4, 0:2, :])
-            pieces[f"g{h}"] = (fut_sb[:, 4 * h : 4 * h + 4, 2:4, :], fut_v[:, 4 * h : 4 * h + 4, 2:4, :])
+            pieces[f"a{h}"] = (fut_sb[h][0][:], fut_v[:, 4 * h : 4 * h + 4, 0:2, :])
+            pieces[f"g{h}"] = (fut_sb[h][1][:], fut_v[:, 4 * h : 4 * h + 4, 2:4, :])
         pieces["r"] = (wres_sb[:], wres.rearrange("(p j) n -> p j n", j=T))
         nc.scalar.dma_start(out=scale_sb[:], in_=w2_scale.rearrange("(g p t) o -> p g (t o)", g=2, t=T))
         nc.scalar.dma_start(out=vp_sb[0:1, :], in_=vp.rearrange("(o n) -> o n", o=1))
@@ -164,7 +175,9 @@ def tile_tideresidualencodertemporaldecoder_kernel(
             wg = w1_tiles[g]
             half = m0 // 64
             o = wg[:, :, m0:m1, :]
-            a = w1_sb[:, :, 512 * g + T * m0 : 512 * g + T * m1].rearrange("p j (m t) -> p t m j", t=T)
+            c0 = 512 * g + T * m0
+            a = w1_lo[:] if c0 == 0 else w1_hi[:, :, c0 - HALF : c0]
+            a = a.rearrange("p j (m t) -> p t m j", t=T)
             if IL_W1[2 * g + half] == "v":
                 nc.vector.tensor_copy(out=o, in_=a)
             elif IL_W1[2 * g + half] == "s":
@@ -247,7 +260,7 @@ def tile_tideresidualencodertemporaldecoder_kernel(
 
             def widen(g):
                 for t in range(T):
-                    fp8 = w2_sb[g][:, t, p * H + j * HALF : p * H + (j + 1) * HALF].bitcast(E4M3)
+                    fp8 = w2_cols(g, t, p, j).bitcast(E4M3)
                     sc = scale_sb[:, g, t : t + 1]
                     if WIDEN[b][g][t] == "s":
                         nc.scalar.activation(out=get("wide")[:, g, t, :], in_=fp8, func=ACT.Copy, scale=sc)
@@ -257,10 +270,10 @@ def tile_tideresidualencodertemporaldecoder_kernel(
             return {
                 "n0": lambda: widen(0),
                 "n1": lambda: widen(1),
-                "k": lambda piece=0: interleave(IL_WSK[b], get("wskg")[:], wsk_sb[:, :, p * H + j * HALF : p * H + (j + 1) * HALF], f"B{b}k", piece),
+                "k": lambda piece=0: interleave(IL_WSK[b], get("wskg")[:], wsk_cols(p, j), f"B{b}k", piece),
                 "i0": lambda piece=0: interleave(IL_W2[b][0], get("w2g")[:, 0], get("wide")[:, 0], f"B{b}i0", piece),
                 "i1": lambda piece=0: interleave(IL_W2[b][1], get("w2g")[:, 1], get("wide")[:, 1], f"B{b}i1", piece),
-                "Tk": lambda: interleave("T", None, wsk_sb[:, :, p * H + j * HALF : p * H + (j + 1) * HALF]),
+                "Tk": lambda: interleave("T", None, wsk_cols(p, j)),
                 "Ti0": lambda: interleave("T", None, get("wide")[:, 0]),
                 "Ti1": lambda: interleave("T", None, get("wide")[:, 1]),
                 "qk": lambda: quantize(wsk_q[j][p], get("wskg")[:].rearrange("p n t -> p (n t)")),
@@ -292,7 +305,7 @@ def tile_tideresidualencodertemporaldecoder_kernel(
                 extra = psum.tile([P, 2, HALF], F32, name="extra", bufs=2)
                 for c in range(2):
                     terms = [
-                        (diag[q], fut_sb[:, 2 * i + c, q, j * HALF : (j + 1) * HALF]) for q in range(NP)
+                        (diag[q], fut_sb[i // 2][q // 2][:, 2 * (i % 2) + c, q % 2, j * HALF : (j + 1) * HALF]) for q in range(NP)
                     ] + [(ndiag[q], kept_m[j, i, q][:, c, :]) for q in PE_P2[j][i]]
                     for n, (weights, moving) in enumerate(terms):
                         nc.tensor.matmul(
@@ -311,7 +324,7 @@ def tile_tideresidualencodertemporaldecoder_kernel(
                 kept_m[j, i, p] = m
             else:
                 m = work.tile([P, 2, HALF], F32, name="m", bufs=6)
-            f = fut_sb[:, 2 * i : 2 * i + 2, p, j * HALF : (j + 1) * HALF]
+            f = fut_sb[i // 2][p // 2][:, 2 * (i % 2) : 2 * (i % 2) + 2, p % 2, j * HALF : (j + 1) * HALF]
             if FORM[j][i]:
                 nc.vector.tensor_tensor(out=m[:], in0=bank[:], in1=f, op=ALU.add)
             else:

from contextlib import ExitStack

import concourse.mybir as mybir
from concourse.masks import make_identity

N, L, F, H, NP = 1024, 512, 1024, 512, 4
FLOPS = 2 * N * (L * F + F * NP * H + L * NP * H + L * H)

F32 = mybir.dt.float32
BF16 = mybir.dt.bfloat16
U32 = mybir.dt.uint32
U8 = mybir.dt.uint8
E4M3 = mybir.dt.float8_e4m3fn
E4M3X4 = mybir.dt.float8_e4m3fn_x4
ALU = mybir.AluOpType
ACT = mybir.ActivationFunctionType

P = 128
T = 4
HALF = 256
PAIRS = N // (2 * P)
FORM = [[0,0,0,0],[0,0,0,0]]
IL_W1 = ["s","v","s","v"]
IL_WSK = ["v","v","s","s","s","s","s","s"]
IL_W2 = [["v","v"],["s","s"],["s","s"],["s","s"],["v","s"],["s","s"],["s","s"],["s","s"]]
IL_WRES = ["v","s"]
H_ENG = [[["s","s"],["s","s"]],[["v","v"],["s","s"]],[["s","s"],["s","s"]],[["s","s"],["s","s"]]]
X_ENG = ["s","s","s","v"]
WIDEN = [["vvvv","vvvv"],["ssss","vvvv"],["ssss","ssss"],["ssss","ssss"],["vvvv","ssss"],["ssss","ssss"],["ssss","ssss"],["ssss","ssss"]]
PE_P2 = [[[1],[2],[],[1]],[[2],[],[],[2]]]
LOADS = "m10 m00 w10 x2 x0 w1b x1 k0 r a0 x3 g1 m11 a1 m01 k1 g0"
ORDER = "B0n1 B4n1 B0i1 B4i1 B0n0 B4n0 X2 w2 B0i0 X0 B4i0 x2 V B0q x0 B4q w4 w3 X1 qx2 qw0 x1 qx0 H200 B4k qx1 H201 B0k H000 H001 w5 H100 h200 H101 B4qk h201 qw1 h000 qh20 H010 h100 D h001 H011 H210 h101 h010 H211 H110 qh00 h011 X3 qh10 h210 B0qk H111 qh01 h211 x3 M0 h110 r0 M16 h111 qx3 qr0 H300 qh11 r1 H301 P0 H310 qh21 H311 P16 W0 h300 M1 B1n1 h301 W1 S0 B1i1 M2 P1 W2 qh30 h310 M17 S1 h311 P2 F02 B2n1 P17 qh31 M18 S2 B3n1 qr1 M3 A02 B1n0 P18 W3 W16 P3 M19 S16 B3i1 S3 P19 W17 B1i0 W18 S17 S18 W19 B3n0 S19 F12 B1k B3k F11 B1q B1qk B3i0 A12 M4 B3qk A11 M5 B5n1 B3q M6 P4 B5n0 P5 M7 P6 B5i1 M12 S5 S6 M13 B5i0 P7 M14 P12 P13 B2k F03 B5q S12 B5k S13 P14 M15 B6k B5qk S14 M20 P15 B2n0 M21 B6qk S15 F00 B2i1 P20 P21 B2i0 S20 S21 M22 B2qk B6n1 B2q M23 P22 B6n0 A03 M8 S22 M9 B6i1 P8 P23 M10 S8 B6i0 M11 P9 P10 F01 B7n1 B6q S10 B7n0 P11 S23 M24 B7i1 S11 M25 P24 B7i0 A00 M26 P25 F10 B7k P26 B7q S25 B7qk M27 S26 A10 M28 P27 M29 A01 P28 M30 P29 M31 S28 S29 F13 P30 P31 S30 S31 A13"
MANUAL = True


def tile_tideresidualencodertemporaldecoder_kernel(
    tc, x, fut, w1, w2_bytes, w2_scale, wsk, vp, wres, out
):
    nc = tc.nc
    with ExitStack() as ctx:
        keep = ctx.enter_context(tc.tile_pool(name="keep", bufs=1))
        work = ctx.enter_context(tc.tile_pool(name="work", bufs=2))
        psum = ctx.enter_context(tc.psum_pool(name="psum", bufs=6))

        x_sb = [keep.tile([P, 2, L], BF16, name=f"x_sb{i}") for i in range(PAIRS)]
        w1_lo = keep.tile([P, T, HALF], BF16, name="w1_lo")
        w1_hi = keep.tile([P, T, F - HALF], BF16, name="w1_hi")
        wsk_lo = keep.tile([P, T, H], BF16, name="wsk_lo")
        wsk_hi = keep.tile([P, T, 3 * H], BF16, name="wsk_hi")
        w2_lo = [keep.tile([P, T, H], U8, name=f"w2_lo{g}") for g in range(2)]
        w2_hi = [keep.tile([P, T, 3 * H], U8, name=f"w2_hi{g}") for g in range(2)]
        wres_sb = keep.tile([P, T, H], BF16, name="wres_sb")
        fut_sb = [[keep.tile([P, 4, 2, H], BF16, name=f"fut_sb{h}{b}") for b in range(2)] for h in range(2)]
        scale_sb = keep.tile([P, 2, T], F32, name="scale_sb")
        vp_sb = keep.tile([P, NP], BF16, name="vp_sb")
        nc.vector.memset(vp_sb[:], 0.0)

        x_v = x.rearrange("(q i c) k -> i q c k", c=2, i=PAIRS)
        w1_v = w1.rearrange("(p j) f -> p j f", j=T)
        wsk_v = wsk.rearrange("(p j) n -> p j n", j=T)
        w2_v = w2_bytes.rearrange("(g p t) n -> g p t n", g=2, t=T)
        fut_v = fut.rearrange("(q c) b n -> q c b n", q=P)

        def load(dst, src):
            nc.sync.dma_start(out=dst, in_=src)

        def wsk_cols(p, j):
            c0 = p * H + j * HALF
            return wsk_lo[:, :, c0 : c0 + HALF] if p == 0 else wsk_hi[:, :, c0 - H : c0 - H + HALF]

        def w2_cols(g, t, p, j):
            c0 = p * H + j * HALF
            return w2_lo[g][:, t, c0 : c0 + HALF] if p == 0 else w2_hi[g][:, t, c0 - H : c0 - H + HALF]

        pieces = {f"x{i}": (x_sb[i][:], x_v[i]) for i in range(PAIRS)}
        pieces["w10"] = (w1_lo[:], w1_v[:, :, 0:HALF])
        pieces["w1b"] = (w1_hi[:], w1_v[:, :, HALF:F])
        pieces["k0"] = (wsk_lo[:], wsk_v[:, :, 0:H])
        pieces["k1"] = (wsk_hi[:], wsk_v[:, :, H : NP * H])
        for g in range(2):
            pieces[f"m{g}0"] = (w2_lo[g][:], w2_v[g][:, :, 0:H])
            pieces[f"m{g}1"] = (w2_hi[g][:], w2_v[g][:, :, H : NP * H])
        for h in range(2):
            pieces[f"a{h}"] = (fut_sb[h][0][:], fut_v[:, 4 * h : 4 * h + 4, 0:2, :])
            pieces[f"g{h}"] = (fut_sb[h][1][:], fut_v[:, 4 * h : 4 * h + 4, 2:4, :])
        pieces["r"] = (wres_sb[:], wres.rearrange("(p j) n -> p j n", j=T))
        nc.scalar.dma_start(out=scale_sb[:], in_=w2_scale.rearrange("(g p t) o -> p g (t o)", g=2, t=T))
        nc.scalar.dma_start(out=vp_sb[0:1, :], in_=vp.rearrange("(o n) -> o n", o=1))
        for k in LOADS.split():
            load(*pieces[k])

        dummy = keep.tile([P, 1], F32, name="dummy")
        nc.gpsimd.memset(dummy[:], 0.0)
        nc.scalar.activation(out=dummy[:], in_=dummy[:], func=ACT.Relu)
        ident_f32 = keep.tile([P, P], F32, name="ident_f32")
        make_identity(nc, ident_f32[:])
        ident = keep.tile([P, P], BF16, name="ident")
        make_identity(nc, ident[:])
        ones = keep.tile([P, P], BF16, name="ones")
        nc.gpsimd.memset(ones[:], 1.0)
        v_col = keep.tile([P, NP], F32, name="v_col")
        nv_col = keep.tile([P, NP], F32, name="nv_col")
        kept_m = {}
        ndiag = {p: keep.tile([P, P], F32, name=f"ndiag{p}") for p in sorted({q for r in PE_P2 for t in r for q in t})}
        diag = [keep.tile([P, P], BF16, name=f"diag{p}") for p in range(NP)]

        def spread_v():
            bank = psum.tile([P, NP], F32, name="extra", bufs=2)
            nc.tensor.matmul(bank[:], lhsT=ones[:], rhs=vp_sb[:], start=True, stop=True)
            nc.scalar.copy(out=v_col[:], in_=bank[:])
            nc.scalar.activation(out=nv_col[:], in_=v_col[:], func=ACT.Copy, scale=-1.0)

        def build_diagonals():
            for p in ndiag:
                nc.gpsimd.tensor_scalar(
                    out=ndiag[p][:], in0=ident_f32[:], scalar1=nv_col[:, p : p + 1], scalar2=0.0, op0=ALU.mult, op1=ALU.add
                )
            for p in range(NP):
                nc.gpsimd.tensor_scalar(
                    out=diag[p][:], in0=ident[:], scalar1=v_col[:, p : p + 1], scalar2=0.0, op0=ALU.mult, op1=ALU.add
                )

        def codes(width, name):
            return (
                keep.tile([P, width], U32, name=name, align_bytes=64),
                keep.tile([P, width], U8, name=name + "_s", align_bytes=64),
            )

        x_q = [codes(2 * P, f"x_q{i}") for i in range(PAIRS)]
        h_q = [[codes(2 * P, f"h_q{i}_{g}") for g in range(2)] for i in range(PAIRS)]
        w1_q = [codes(512, f"w1_q{g}") for g in range(2)]
        wres_q = [codes(HALF, f"wres_q{j}") for j in range(2)]
        wsk_q = [[codes(HALF, f"wsk_q{j}_{p}") for p in range(NP)] for j in range(2)]
        w2_q = [[codes(2 * HALF, f"w2_q{j}_{p}") for p in range(NP)] for j in range(2)]

        def quantize(dst, src):
            nc.vector.quantize_mx(out=dst[0][:].bitcast(E4M3X4), scales=dst[1][:], in_=src)

        def mm(out_ap, a, a0, b, b0, n, start, stop):
            nc.tensor.matmul_mx(
                out=out_ap,
                lhsT=a[0][:, a0 : a0 + P].bitcast(E4M3X4),
                lhsT_scale=a[1][:, a0 : a0 + P],
                rhs=b[0][:, b0 : b0 + n].bitcast(E4M3X4),
                rhs_scale=b[1][:, b0 : b0 + n],
                start=start,
                stop=stop,
            )

        later = {}

        x_banks, h_banks = {}, {}

        def turn_x(i):
            bank = x_banks[i] = psum.tile([P, 2, 2, P], F32, name="bank")
            for c in range(2):
                words = x_sb[i][:, c, :].bitcast(F32)
                for u in range(2):
                    nc.tensor.transpose(bank[:, c, u, :], words[:, u::2], ident_f32[:])

        def copy_x(i):
            bank = x_banks[i]
            xg = work.tile([P, 2, P, T], BF16, name="xg", align_bytes=64, bufs=4)
            (nc.scalar.copy if X_ENG[i] == "s" else nc.vector.tensor_copy)(
                out=xg[:].rearrange("p c n t -> p (c n t)").bitcast(F32).rearrange("p (c n u) -> p c n u", c=2, u=2),
                in_=bank[:].rearrange("p c u n -> p c n u"),
            )
            later[f"x{i}"] = lambda: quantize(x_q[i], xg[:].rearrange("p c n t -> p (c n t)"))

        w1_tiles = {}

        def prep_w1(g, m0, m1, piece=0):
            if g not in w1_tiles:
                w1_tiles[g] = work.tile([P, T, P, T], BF16, name="w1g", align_bytes=64)
            wg = w1_tiles[g]
            half = m0 // 64
            o = wg[:, :, m0:m1, :]
            c0 = 512 * g + T * m0
            a = w1_lo[:] if c0 == 0 else w1_hi[:, :, c0 - HALF : c0]
            a = a.rearrange("p j (m t) -> p t m j", t=T)
            if IL_W1[2 * g + half] == "v":
                nc.vector.tensor_copy(out=o, in_=a)
            elif IL_W1[2 * g + half] == "s":
                nc.scalar.copy(out=o, in_=a)
            else:
                for u0, u1 in [((0, 22), (22, 43), (43, 64))[piece]]:
                    nc.gpsimd.tensor_scalar(out=o[:, :, u0:u1], in0=a[:, :, u0:u1], scalar1=1.0, scalar2=0.0, op0=ALU.mult, op1=ALU.add)
            later[f"w{g}"] = lambda: quantize(w1_q[g], wg[:].rearrange("p t m j -> p (t m j)"))

        def hidden(i, g, c):
            if True:
                bank = h_banks[i, g, c] = psum.tile([P, T, P], F32, name="bank")
                for t in range(T):
                    mm(bank[:, t, :], w1_q[g], t * P, x_q[i], c * P, P, True, True)

        h_tiles = {}

        def copy_h(i, g, c):
            if (i, g) not in h_tiles:
                h_tiles[i, g] = work.tile([P, 2, P, T], BF16, name="hg", align_bytes=64, bufs=6)
                later[f"h{i}{g}"] = lambda: quantize(h_q[i][g], h_tiles[i, g][:].rearrange("p c n t -> p (c n t)"))
            hg = h_tiles[i, g]
            if True:
                bank = h_banks[i, g, c]
                if H_ENG[i][g][c] == "s":
                    nc.scalar.activation(out=hg[:, c], in_=bank[:].rearrange("p t n -> p n t"), func=ACT.Relu)
                else:
                    nc.vector.tensor_scalar(out=hg[:, c], in0=bank[:].rearrange("p t n -> p n t"), scalar1=0.0, scalar2=None, op0=ALU.max)

        spread_banks = {}

        def interleave(engine, dst, src, key=None, piece=0):
            if engine == "T":
                bank = psum.tile([P, HALF, T], BF16, name="bank")
                for n0 in range(0, HALF, P):
                    nc.tensor.matmul(
                        bank[:, n0 : n0 + P, :].rearrange("p n j -> p (n j)"),
                        lhsT=ident[:],
                        rhs=src[:, :, n0 : n0 + P].rearrange("p j n -> p n j"),
                        start=True,
                        stop=True,
                    )
                return bank
            elif engine == "pe":
                nc.scalar.copy(out=dst, in_=spread_banks[key][:])
            else:
                cuts = [0, 88, 172, HALF] if engine == "g" else [0, HALF]
                for n0, n1 in [(cuts[piece], cuts[piece + 1])]:
                    part = slice(n0, n1)
                    o = dst[:, part].rearrange("p (c i) j -> p c j i", i=4)
                    a = src[:, :, part].rearrange("p j (c i) -> p c j i", i=4)
                    if engine == "g":
                        nc.gpsimd.tensor_scalar(out=dst[:, part], in0=src[:, :, part].rearrange("p j n -> p n j"), scalar1=1.0, scalar2=0.0, op0=ALU.mult, op1=ALU.add)
                    elif engine == "v":
                        nc.vector.tensor_copy(out=o, in_=a)
                    else:
                        nc.scalar.copy(out=o, in_=a)

        wres_tiles = {}

        def prep_wres(j, piece=0):
            if j not in wres_tiles:
                wres_tiles[j] = work.tile([P, HALF, T], BF16, name="wresg", align_bytes=64, bufs=1)
            wg = wres_tiles[j]
            interleave(IL_WRES[j], wg[:], wres_sb[:, :, j * HALF : (j + 1) * HALF], f"r{j}", piece)
            later[f"r{j}"] = lambda: quantize(wres_q[j], wg[:].rearrange("p n t -> p (n t)"))

        blocks = [(j, p) for j in range(2) for p in range(NP)]

        def prep_block(b):
            j, p = blocks[b]
            made = {}

            def get(name):
                if name not in made:
                    shape = {"wide": [P, 2, T, HALF], "w2g": [P, 2, HALF, T], "wskg": [P, HALF, T]}[name]
                    made[name] = work.tile(shape, BF16, name=name, align_bytes=64, bufs=3)
                return made[name]


            def widen(g):
                for t in range(T):
                    fp8 = w2_cols(g, t, p, j).bitcast(E4M3)
                    sc = scale_sb[:, g, t : t + 1]
                    if WIDEN[b][g][t] == "s":
                        nc.scalar.activation(out=get("wide")[:, g, t, :], in_=fp8, func=ACT.Copy, scale=sc)
                    else:
                        nc.vector.tensor_scalar(out=get("wide")[:, g, t, :], in0=fp8, scalar1=sc, scalar2=None, op0=ALU.mult)

            return {
                "n0": lambda: widen(0),
                "n1": lambda: widen(1),
                "k": lambda piece=0: interleave(IL_WSK[b], get("wskg")[:], wsk_cols(p, j), f"B{b}k", piece),
                "i0": lambda piece=0: interleave(IL_W2[b][0], get("w2g")[:, 0], get("wide")[:, 0], f"B{b}i0", piece),
                "i1": lambda piece=0: interleave(IL_W2[b][1], get("w2g")[:, 1], get("wide")[:, 1], f"B{b}i1", piece),
                "Tk": lambda: interleave("T", None, wsk_cols(p, j)),
                "Ti0": lambda: interleave("T", None, get("wide")[:, 0]),
                "Ti1": lambda: interleave("T", None, get("wide")[:, 1]),
                "qk": lambda: quantize(wsk_q[j][p], get("wskg")[:].rearrange("p n t -> p (n t)")),
                "q": lambda: quantize(w2_q[j][p], get("w2g")[:].rearrange("p g n t -> p (g n t)")),
            }

        acc = [[keep.tile([P, 2, HALF], F32, name=f"acc{j}_{i}") for i in range(PAIRS)] for j in range(2)]
        flat = "p c n -> p (c n)"

        def multiply(b, i):
            j, p = blocks[b]
            bank = psum.tile([P, 2, HALF], F32, name="bank")
            for c in range(2):
                mm(bank[:, c, :], x_q[i], c * P, wsk_q[j][p], 0, HALF, True, False)
                mm(bank[:, c, :], h_q[i][0], c * P, w2_q[j][p], 0, HALF, False, False)
                mm(bank[:, c, :], h_q[i][1], c * P, w2_q[j][p], HALF, HALF, False, True)
            return bank

        def skip_product(b, i):
            j, p = blocks[b]
            if True:
                extra = psum.tile([P, 2, HALF], F32, name="extra", bufs=2)
                for c in range(2):
                    mm(extra[:, c, :], x_q[i], c * P, wres_q[j], 0, HALF, True, True)
            return extra

        def sf_group(j, i):
            if True:
                extra = psum.tile([P, 2, HALF], F32, name="extra", bufs=2)
                for c in range(2):
                    terms = [
                        (diag[q], fut_sb[i // 2][q // 2][:, 2 * (i % 2) + c, q % 2, j * HALF : (j + 1) * HALF]) for q in range(NP)
                    ] + [(ndiag[q], kept_m[j, i, q][:, c, :]) for q in PE_P2[j][i]]
                    for n, (weights, moving) in enumerate(terms):
                        nc.tensor.matmul(
                            extra[:, c, :],
                            lhsT=weights[:],
                            rhs=moving,
                            start=(n == 0),
                            stop=(n == len(terms) - 1),
                        )
            return extra

        def first_pass(b, i, bank):
            j, p = blocks[b]
            if p in PE_P2[j][i]:
                m = work.tile([P, 2, HALF], F32, name="m_kept", bufs=4)
                kept_m[j, i, p] = m
            else:
                m = work.tile([P, 2, HALF], F32, name="m", bufs=6)
            f = fut_sb[i // 2][p // 2][:, 2 * (i % 2) : 2 * (i % 2) + 2, p % 2, j * HALF : (j + 1) * HALF]
            if FORM[j][i]:
                nc.vector.tensor_tensor(out=m[:], in0=bank[:], in1=f, op=ALU.add)
            else:
                nc.vector.scalar_tensor_tensor(out=m[:], in0=bank[:], scalar=-1.0, in1=f, op0=ALU.mult, op1=ALU.min)
            return m

        def finish(j, i):
            left[j, i] -= 1
            if left[j, i] == 0:
                nc.sync.dma_start(
                    out=out.rearrange("(q i c) (j n) -> i j q c n", c=2, i=PAIRS, j=2)[i, j], in_=acc[j][i][:]
                )

        left = {(j, i): 4 if FORM[j][i] else 5 - len(PE_P2[j][i]) for j in range(2) for i in range(PAIRS)}

        def add_sf(j, i, extra):
            a = acc[j][i]
            nc.vector.tensor_tensor(out=a[:], in0=a[:], in1=extra[:], op=ALU.add)
            finish(j, i)

        def second_pass(b, i, m, extra):
            j, p = blocks[b]
            a = acc[j][i]
            if p in PE_P2[j][i]:
                return
            nc.vector.scalar_tensor_tensor(
                out=a[:],
                in0=m[:],
                scalar=(v_col if FORM[j][i] else nv_col)[:, p : p + 1],
                in1=extra[:] if p == 0 else a[:],
                op0=ALU.mult,
                op1=ALU.add,
            )
            finish(j, i)

        steps = [(b, i) for b in range(len(blocks)) for i in range(PAIRS)]
        banks, extras, ms = {}, {}, {}
        preps = {}
        kept = {}

        def emit(k):
            kind, n = k[0], k[1:]
            if kind == "g":
                piece = int(n[0])
                if n[1] == "B":
                    b = int(n[2])
                    if b not in preps:
                        preps[b] = prep_block(b)
                    preps[b][n[3:]](piece)
                elif n[1] == "r":
                    prep_wres(int(n[2]), piece)
                else:
                    q = int(n[2])
                    prep_w1((q - 2) // 2, 64 * (q % 2), 64 * (q % 2) + 64, piece)
                return
            if kind == "B":
                b = int(n[0])
                if b not in preps:
                    preps[b] = prep_block(b)
                preps[b][n[1:]]()
            elif kind == "q":
                later[n]()
            elif kind == "x":
                copy_x(int(n))
            elif kind == "X":
                turn_x(int(n))
            elif kind == "w":
                prep_w1((int(n) - 2) // 2, 64 * (int(n) % 2), 64 * (int(n) % 2) + 64)
            elif kind == "r":
                prep_wres(int(n))
            elif kind == "h":
                copy_h(int(n[0]), int(n[1]), int(n[2]))
            elif kind == "H":
                hidden(int(n[0]), int(n[1]), int(n[2]))
            elif kind == "V":
                spread_v()
            elif kind == "D":
                build_diagonals()
            elif kind == "M":
                banks[int(n)] = multiply(*steps[int(n)])
            elif kind == "W":
                extras[int(n)] = skip_product(*steps[int(n)])
            elif kind == "T":
                if n[0] == "r":
                    j = int(n[1])
                    spread_banks[n] = interleave("T", None, wres_sb[:, :, j * HALF : (j + 1) * HALF])
                else:
                    b = int(n[1])
                    if b not in preps:
                        preps[b] = prep_block(b)
                    spread_banks[n] = preps[b]["T" + n[2:]]()
            elif kind == "P":
                ms[int(n)] = first_pass(*steps[int(n)], banks[int(n)])
            elif kind == "R":
                nc.scalar.activation(out=ms[int(n)][:], in_=ms[int(n)][:], func=ACT.Relu)
            elif kind == "S":
                second_pass(*steps[int(n)], ms[int(n)], extras.get(int(n)))
            elif kind == "F":
                kept[n] = sf_group(int(n[0]), int(n[1]))
            elif kind == "A":
                add_sf(int(n[0]), int(n[1]), kept[n])

        if MANUAL:
            ctx.enter_context(tc.manual_schedule())
        for k in ORDER.split():
            emit(k)
